import numpy as np
import ml_dtypes


def mxq(x, axis, fmt="e4m3"):
    dtype, down = {"e4m3": (ml_dtypes.float8_e4m3fn, 7), "e5m2": (ml_dtypes.float8_e5m2, 14)}[fmt]
    v = np.moveaxis(np.asarray(x, np.float32).astype(ml_dtypes.bfloat16).astype(np.float64), axis, -1)
    blocks = v.reshape(v.shape[:-1] + (-1, 32))
    amax = np.abs(blocks).max(-1, keepdims=True)
    byte = np.maximum(np.where(amax > 0, np.frexp(amax)[1] - 1 + 127, 0) - down, 1)
    scale = np.exp2(byte - 127.0)
    codes = (blocks / scale).astype(np.float32).astype(dtype).astype(np.float64)
    return np.moveaxis((codes * scale).reshape(v.shape), -1, axis)


WIDE = False


def mx_kscale(k):
    if not WIDE:
        return np.ones(k)
    levels = np.array([10, -10, 5, -5, 0])
    if k % 512:
        return np.exp2(np.random.permutation(np.resize(levels, k // 32))).repeat(32)
    a = np.empty((k // 512, 16))
    for p in range(k // 512):
        a[p, :8] = np.random.permutation(np.resize(levels, 8))
        for g in range(8):
            far = levels[np.abs(levels - a[p, g]) >= 10]
            a[p, g + 8] = far[np.random.randint(len(far))]
    return np.exp2(a.ravel()).repeat(32)


def f64(x):
    return np.asarray(x).astype(np.float64)


def striped(idx):
    return np.tile(idx.reshape(-1, 16).T, (8, 1)).astype(np.uint16)


def unstriped(offs):
    return offs[:16].T.reshape(-1).astype(np.int64)


E2M1 = np.array([0.0, 0.5, 1.0, 1.5, 2.0, 3.0, 4.0, 6.0, -0.0, -0.5, -1.0, -1.5, -2.0, -3.0, -4.0, -6.0])


def pack_weight(w, fmt):
    k, n = w.shape
    w = f64(np.asarray(w, np.float32).astype(ml_dtypes.bfloat16)).reshape(k // 32, 32, n)
    amax = np.abs(w).max(1)
    if fmt == "e4m3":
        byte = np.frexp(amax)[1] - 1 + 127 - 7
    else:
        mant, ex = np.frexp(amax / 6.0)
        byte = np.where(mant > 0.5, ex, ex - 1) + 127
    byte = np.clip(np.where(amax > 0, byte, 1), 1, 254)
    scaled = (w * np.exp2(127.0 - byte)[:, None, :]).reshape(k, n).astype(np.float32)
    by_word = np.ascontiguousarray(scaled.reshape(k // 512, 128, 4, n).transpose(0, 1, 3, 2))
    if fmt == "e4m3":
        words = by_word.astype(ml_dtypes.float8_e4m3fn).view(np.uint8)
    else:
        c = by_word.astype(ml_dtypes.float4_e2m1fn).view(np.uint8) & 0xF
        words = (c[..., 0::2] | (c[..., 1::2] << 4)).reshape(k // 512, 128, 2 * n)
    return np.ascontiguousarray(words), np.ascontiguousarray(byte.astype(np.uint8).reshape(k // 512, 16, n))


def unpack_weight(words, scales, fmt):
    g, _, n = scales.shape
    words = np.ascontiguousarray(words).reshape(g, 128, n, -1)
    if fmt == "e4m3":
        vals = words.view(ml_dtypes.float8_e4m3fn).astype(np.float64)
    else:
        nib = np.empty((g, 128, n, 4), np.uint8)
        nib[..., 0::2] = words & 0xF
        nib[..., 1::2] = words >> 4
        vals = E2M1[nib]
    vals = vals * np.repeat(np.exp2(scales.astype(np.float64) - 127.0), 8, axis=1)[..., None]
    return vals.transpose(0, 1, 3, 2).reshape(g * 512, n)


def silu(v):
    return v / (1.0 + np.exp(-np.maximum(v, -700.0)))


K, M, T, S = 512, 512, 2048, 1024


def setup_inputs():
    n = np.random.standard_normal
    s = mx_kscale(K)[:, None]
    s2 = mx_kscale(512)[:, None]
    v = pack_weight(n((K, T)) * s, "e4m3")
    p_w4 = pack_weight(n((K, M)) / np.sqrt(K) / s, "e2m1")
    return {
        "tab_words": v[0],
        "tab_scales": v[1],
        "w4_words": p_w4[0],
        "w4_scales": p_w4[1],
        "c": (n((512, S)) * s2).astype(np.float32),
        "u": (n((512, M)) / np.sqrt(512) / s2).astype(np.float32),
        "gT": n((M, T)).astype(np.float32),
        "b": (0.3 * n(512)).astype(np.float32),
        "offs": striped(np.random.permutation(T)[:S]),
    }


def reference(tab_words, tab_scales, w4_words, w4_scales, c, u, gT, b, offs):
    tab_ = unpack_weight(tab_words, tab_scales, "e4m3")[:, unstriped(offs)]
    w4_ = unpack_weight(w4_words, w4_scales, "e2m1")
    c_ = mxq(f64(c), 0, "e4m3")
    u_ = mxq(f64(u), 0, "e4m3")
    y = w4_.T @ tab_ + u_.T @ c_
    return (silu(y + f64(b)[:, None])) * f64(gT)[:, unstriped(offs)]

@@ -1,0 +1,142 @@
+from contextlib import ExitStack
+
+import concourse.mybir as mybir
+
+K, M, T, S = 512, 512, 2048, 1024
+FLOPS = 2 * 2 * K * M * S
+
+F32 = mybir.dt.float32
+BF16 = mybir.dt.bfloat16
+I32 = mybir.dt.int32
+U32 = mybir.dt.uint32
+U16 = mybir.dt.uint16
+U8 = mybir.dt.uint8
+FP8X4 = mybir.dt.float8_e4m3fn_x4
+FP4X4 = mybir.dt.float4_e2m1fn_x4
+SILU = mybir.ActivationFunctionType.Silu
+MULT = mybir.AluOpType.mult
+
+P = 128
+PACK = 4
+HALF = 512
+M_TILES = M // P
+PER_COL = 16
+U_SCALAR_COLS = 256
+C1_SCALAR_COLS = 192
+LAST_PIECES = (512, 256, 256)
+
+
+def load_scale_rows(nc, plane, rows):
+    for q in range(4):
+        nc.sync.dma_start(out=plane[32 * q : 32 * q + 4, :], in_=rows[4 * q : 4 * q + 4, :].bitcast(I32))
+
+
+def interleave(nc, grouped, raw, scalar_cols):
+    width = raw.shape[2]
+    if scalar_cols > 0:
+        nc.scalar.copy(out=grouped[:, :scalar_cols, :], in_=raw[:, :, :scalar_cols].rearrange("p j w -> p w j"))
+    if scalar_cols < width:
+        nc.vector.tensor_copy(out=grouped[:, scalar_cols:, :], in_=raw[:, :, scalar_cols:].rearrange("p j w -> p w j"))
+
+
+def quantize(nc, codes, scales, grouped):
+    nc.vector.quantize_mx(out=codes[:].bitcast(FP8X4), scales=scales[:], in_=grouped[:].rearrange("p w j -> p (w j)"))
+
+
+def tile_list_tabgate_silu_kernel(tc, tab_words, tab_scales, w4_words, w4_scales, c, u, gT, b, offs, out):
+    nc = tc.nc
+    with ExitStack() as ctx:
+        keep = ctx.enter_context(tc.tile_pool(name="keep", bufs=1))
+        psum = ctx.enter_context(tc.psum_pool(name="psum", bufs=1))
+
+        offsets = keep.tile([P, S // PER_COL], U16, name="offsets")
+        tab_w = keep.tile([P, T], I32, name="tab_w", align_bytes=64)
+        tab_s = keep.tile([P, T // 4], I32, name="tab_s", align_bytes=64)
+        w4_w = keep.tile([P, M // 2], I32, name="w4_w", align_bytes=64)
+        w4_s = keep.tile([P, M // 4], I32, name="w4_s", align_bytes=64)
+        bias = keep.tile([P, M_TILES], F32, name="bias")
+        warm = keep.tile([P, 1], F32, name="warm")
+        c_raw = [keep.tile([P, PACK, HALF], F32, name="c_raw%d" % h) for h in range(2)]
+        u_raw = keep.tile([P, PACK, M], F32, name="u_raw")
+        gates = [keep.tile([P, T], F32, name="gates%d" % m) for m in range(M_TILES)]
+
+        nc.vector.memset(tab_s[:], 0)
+        nc.vector.memset(w4_s[:], 0)
+
+        c_rows = c.rearrange("(p j) s -> p j s", j=PACK)
+        nc.sync.dma_start(offsets[:], offs)
+        nc.sync.dma_start(out=tab_w[:], in_=tab_words[0].rearrange("p t i -> p (t i)").bitcast(I32))
+        with nc.allow_non_contiguous_dma(reason="one bias value a partition"):
+            nc.gpsimd.dma_start(out=bias[:], in_=b.rearrange("(m p) -> p m", p=P))
+        nc.gpsimd.dma_start(out=w4_w[:], in_=w4_words[0].bitcast(I32))
+        load_scale_rows(nc, tab_s, tab_scales[0])
+        nc.sync.dma_start(out=c_raw[0][:], in_=c_rows[:, :, :HALF])
+        nc.sync.dma_start(out=u_raw[:], in_=u.rearrange("(p j) n -> p j n", j=PACK))
+        load_scale_rows(nc, w4_s, w4_scales[0])
+        nc.sync.dma_start(out=c_raw[1][:], in_=c_rows[:, :, HALF:])
+        for m in range(M_TILES):
+            nc.sync.dma_start(out=gates[m][:], in_=gT[m * P : (m + 1) * P, :])
+
+        nc.scalar.activation(out=warm[:], in_=bias[:, 0:1], func=SILU)
+
+        v_codes = keep.tile([P, S], U32, name="v_codes", align_bytes=64)
+        v_scales = keep.tile([P, S], U8, name="v_scales", align_bytes=64)
+        nc.vector.tensor_copy(v_codes[:], tab_w[:].bitcast(U32).indirect(offsets[:]))
+        nc.vector.tensor_copy(v_scales[:], tab_s[:].bitcast(U8).indirect(offsets[:]))
+
+        c_bf = [keep.tile([P, HALF, PACK], BF16, name="c_bf%d" % h, align_bytes=64) for h in range(2)]
+        c_codes = [keep.tile([P, HALF], U32, name="c_codes%d" % h, align_bytes=64) for h in range(2)]
+        c_scales = [keep.tile([P, HALF], U8, name="c_scales%d" % h, align_bytes=64) for h in range(2)]
+        u_bf = keep.tile([P, M, PACK], BF16, name="u_bf", align_bytes=64)
+        u_codes = keep.tile([P, M], U32, name="u_codes", align_bytes=64)
+        u_scales = keep.tile([P, M], U8, name="u_scales", align_bytes=64)
+
+        interleave(nc, c_bf[0], c_raw[0], HALF)
+        interleave(nc, u_bf, u_raw, U_SCALAR_COLS)
+        quantize(nc, c_codes[0], c_scales[0], c_bf[0])
+        quantize(nc, u_codes, u_scales, u_bf)
+        interleave(nc, c_bf[1], c_raw[1], C1_SCALAR_COLS)
+        quantize(nc, c_codes[1], c_scales[1], c_bf[1])
+
+        w4_bytes = w4_w[:].bitcast(U8)
+        w4_scale_bytes = w4_s[:].bitcast(U8)
+        acc = [[psum.tile([P, HALF], F32, name="acc%d_%d" % (m, h)) for h in range(2)] for m in range(M_TILES)]
+        for h in range(2):
+            cols = slice(h * HALF, (h + 1) * HALF)
+            for m in range(M_TILES):
+                rows = slice(m * P, (m + 1) * P)
+                nc.tensor.matmul_mx(
+                    out=acc[m][h][:],
+                    lhsT=w4_bytes[:, 2 * m * P : 2 * (m + 1) * P].bitcast(FP4X4),
+                    lhsT_scale=w4_scale_bytes[:, rows],
+                    rhs=v_codes[:, cols].bitcast(FP8X4),
+                    rhs_scale=v_scales[:, cols],
+                    start=True,
+                    stop=False,
+                )
+                nc.tensor.matmul_mx(
+                    out=acc[m][h][:],
+                    lhsT=u_codes[:, rows].bitcast(FP8X4),
+                    lhsT_scale=u_scales[:, rows],
+                    rhs=c_codes[h][:].bitcast(FP8X4),
+                    rhs_scale=c_scales[h][:],
+                    start=False,
+                    stop=True,
+                )
+
+        for m in range(M_TILES):
+            act = keep.tile([P, S], F32, name="act%d" % m)
+            res = keep.tile([P, S], F32, name="res%d" % m)
+            for h in range(2):
+                nc.scalar.activation(out=act[:, h * HALF : (h + 1) * HALF], in_=acc[m][h][:], func=SILU, bias=bias[:, m : m + 1])
+            pieces = LAST_PIECES if m == M_TILES - 1 else (HALF, HALF)
+            j0 = 0
+            for width in pieces:
+                cols = slice(j0, j0 + width)
+                picked = gates[m][:].indirect(offsets[:, j0 // PER_COL : (j0 + width) // PER_COL])
+                nc.vector.tensor_tensor(res[:, cols], picked, act[:, cols], MULT)
+                if m == M_TILES - 1:
+                    nc.sync.dma_start(out=out[m * P : (m + 1) * P, cols], in_=res[:, cols])
+                j0 += width
+            if m < M_TILES - 1:
+                nc.sync.dma_start(out=out[m * P : (m + 1) * P, :], in_=res[:])

@@ -21,9 +21,7 @@ PACK = 4
 HALF = 512
 M_TILES = M // P
 PER_COL = 16
-U_SCALAR_COLS = 256
-C1_SCALAR_COLS = 192
-LAST_PIECES = (512, 256, 256)
+PIECES = ((512, 512), (1024,), (1024,), (512, 256, 256))
 
 
 def load_scale_rows(nc, plane, rows):
@@ -31,23 +29,21 @@ def load_scale_rows(nc, plane, rows):
         nc.sync.dma_start(out=plane[32 * q : 32 * q + 4, :], in_=rows[4 * q : 4 * q + 4, :].bitcast(I32))
 
 
-def interleave(nc, grouped, raw, scalar_cols):
-    width = raw.shape[2]
-    if scalar_cols > 0:
-        nc.scalar.copy(out=grouped[:, :scalar_cols, :], in_=raw[:, :, :scalar_cols].rearrange("p j w -> p w j"))
-    if scalar_cols < width:
-        nc.vector.tensor_copy(out=grouped[:, scalar_cols:, :], in_=raw[:, :, scalar_cols:].rearrange("p j w -> p w j"))
+def interleave(copy, grouped, raw, cols):
+    copy(out=grouped[:, cols, :], in_=raw[:, :, cols].rearrange("p j w -> p w j"))
 
 
-def quantize(nc, codes, scales, grouped):
-    nc.vector.quantize_mx(out=codes[:].bitcast(FP8X4), scales=scales[:], in_=grouped[:].rearrange("p w j -> p (w j)"))
+def quantize(nc, codes, scales, grouped, cols):
+    nc.vector.quantize_mx(
+        out=codes[:, cols].bitcast(FP8X4), scales=scales[:, cols], in_=grouped[:, cols, :].rearrange("p w j -> p (w j)")
+    )
 
 
 def tile_list_tabgate_silu_kernel(tc, tab_words, tab_scales, w4_words, w4_scales, c, u, gT, b, offs, out):
     nc = tc.nc
     with ExitStack() as ctx:
         keep = ctx.enter_context(tc.tile_pool(name="keep", bufs=1))
-        psum = ctx.enter_context(tc.psum_pool(name="psum", bufs=1))
+        psum = ctx.enter_context(tc.psum_pool(name="psum", bufs=4))
 
         offsets = keep.tile([P, S // PER_COL], U16, name="offsets")
         tab_w = keep.tile([P, T], I32, name="tab_w", align_bytes=64)
@@ -67,13 +63,13 @@ def tile_list_tabgate_silu_kernel(tc, tab_words, tab_scales, w4_words, w4_scales
         nc.sync.dma_start(offsets[:], offs)
         nc.sync.dma_start(out=tab_w[:], in_=tab_words[0].rearrange("p t i -> p (t i)").bitcast(I32))
         with nc.allow_non_contiguous_dma(reason="one bias value a partition"):
-            nc.gpsimd.dma_start(out=bias[:], in_=b.rearrange("(m p) -> p m", p=P))
-        nc.gpsimd.dma_start(out=w4_w[:], in_=w4_words[0].bitcast(I32))
+            nc.scalar.dma_start(out=bias[:], in_=b.rearrange("(m p) -> p m", p=P))
         load_scale_rows(nc, tab_s, tab_scales[0])
         nc.sync.dma_start(out=c_raw[0][:], in_=c_rows[:, :, :HALF])
-        nc.sync.dma_start(out=u_raw[:], in_=u.rearrange("(p j) n -> p j n", j=PACK))
-        load_scale_rows(nc, w4_s, w4_scales[0])
         nc.sync.dma_start(out=c_raw[1][:], in_=c_rows[:, :, HALF:])
+        nc.sync.dma_start(out=w4_w[:], in_=w4_words[0].bitcast(I32))
+        load_scale_rows(nc, w4_s, w4_scales[0])
+        nc.sync.dma_start(out=u_raw[:], in_=u.rearrange("(p j) n -> p j n", j=PACK))
         for m in range(M_TILES):
             nc.sync.dma_start(out=gates[m][:], in_=gT[m * P : (m + 1) * P, :])
 
@@ -91,22 +87,29 @@ def tile_list_tabgate_silu_kernel(tc, tab_words, tab_scales, w4_words, w4_scales
         u_codes = keep.tile([P, M], U32, name="u_codes", align_bytes=64)
         u_scales = keep.tile([P, M], U8, name="u_scales", align_bytes=64)
 
-        interleave(nc, c_bf[0], c_raw[0], HALF)
-        interleave(nc, u_bf, u_raw, U_SCALAR_COLS)
-        quantize(nc, c_codes[0], c_scales[0], c_bf[0])
-        quantize(nc, u_codes, u_scales, u_bf)
-        interleave(nc, c_bf[1], c_raw[1], C1_SCALAR_COLS)
-        quantize(nc, c_codes[1], c_scales[1], c_bf[1])
+        interleave(nc.scalar.copy, c_bf[0], c_raw[0], slice(0, HALF))
+        quantize(nc, c_codes[0], c_scales[0], c_bf[0], slice(0, HALF))
+        interleave(nc.scalar.copy, c_bf[1], c_raw[1], slice(0, 256))
+        interleave(nc.vector.tensor_copy, c_bf[1], c_raw[1], slice(256, HALF))
+        quantize(nc, c_codes[1], c_scales[1], c_bf[1], slice(0, HALF))
+        interleave(nc.vector.tensor_copy, u_bf, u_raw, slice(0, P))
+        interleave(nc.vector.tensor_copy, u_bf, u_raw, slice(P, 2 * P))
+        interleave(nc.scalar.copy, u_bf, u_raw, slice(2 * P, M))
+        quantize(nc, u_codes, u_scales, u_bf, slice(0, P))
+        quantize(nc, u_codes, u_scales, u_bf, slice(P, 2 * P))
+        quantize(nc, u_codes, u_scales, u_bf, slice(2 * P, M))
 
         w4_bytes = w4_w[:].bitcast(U8)
         w4_scale_bytes = w4_s[:].bitcast(U8)
-        acc = [[psum.tile([P, HALF], F32, name="acc%d_%d" % (m, h)) for h in range(2)] for m in range(M_TILES)]
-        for h in range(2):
-            cols = slice(h * HALF, (h + 1) * HALF)
-            for m in range(M_TILES):
-                rows = slice(m * P, (m + 1) * P)
+        for m in range(M_TILES):
+            rows = slice(m * P, (m + 1) * P)
+            act = keep.tile([P, S], F32, name="act%d" % m)
+            res = keep.tile([P, S], F32, name="res%d" % m)
+            for h in range(2):
+                cols = slice(h * HALF, (h + 1) * HALF)
+                acc = psum.tile([P, HALF], F32, name="acc")
                 nc.tensor.matmul_mx(
-                    out=acc[m][h][:],
+                    out=acc[:],
                     lhsT=w4_bytes[:, 2 * m * P : 2 * (m + 1) * P].bitcast(FP4X4),
                     lhsT_scale=w4_scale_bytes[:, rows],
                     rhs=v_codes[:, cols].bitcast(FP8X4),
@@ -115,7 +118,7 @@ def tile_list_tabgate_silu_kernel(tc, tab_words, tab_scales, w4_words, w4_scales
                     stop=False,
                 )
                 nc.tensor.matmul_mx(
-                    out=acc[m][h][:],
+                    out=acc[:],
                     lhsT=u_codes[:, rows].bitcast(FP8X4),
                     lhsT_scale=u_scales[:, rows],
                     rhs=c_codes[h][:].bitcast(FP8X4),
@@ -123,20 +126,14 @@ def tile_list_tabgate_silu_kernel(tc, tab_words, tab_scales, w4_words, w4_scales
                     start=False,
                     stop=True,
                 )
-
-        for m in range(M_TILES):
-            act = keep.tile([P, S], F32, name="act%d" % m)
-            res = keep.tile([P, S], F32, name="res%d" % m)
-            for h in range(2):
-                nc.scalar.activation(out=act[:, h * HALF : (h + 1) * HALF], in_=acc[m][h][:], func=SILU, bias=bias[:, m : m + 1])
-            pieces = LAST_PIECES if m == M_TILES - 1 else (HALF, HALF)
+                nc.scalar.activation(out=act[:, cols], in_=acc[:], func=SILU, bias=bias[:, m : m + 1])
             j0 = 0
-            for width in pieces:
+            for width in PIECES[m]:
                 cols = slice(j0, j0 + width)
                 picked = gates[m][:].indirect(offsets[:, j0 // PER_COL : (j0 + width) // PER_COL])
                 nc.vector.tensor_tensor(res[:, cols], picked, act[:, cols], MULT)
                 if m == M_TILES - 1:
-                    nc.sync.dma_start(out=out[m * P : (m + 1) * P, cols], in_=res[:, cols])
+                    nc.sync.dma_start(out=out[rows, cols], in_=res[:, cols])
                 j0 += width
             if m < M_TILES - 1:
-                nc.sync.dma_start(out=out[m * P : (m + 1) * P, :], in_=res[:])
+                nc.sync.dma_start(out=out[rows, :], in_=res[:])

@@ -1,6 +1,7 @@
 from contextlib import ExitStack
 
 import concourse.mybir as mybir
+from concourse.masks import make_identity
 
 K, M, T, S = 512, 512, 2048, 1024
 FLOPS = 2 * 2 * K * M * S
@@ -25,12 +26,15 @@ PIECES = ((512, 512), (1024,), (1024,), (512, 256, 256))
 
 
 def load_scale_rows(nc, plane, rows):
-    for q in range(4):
-        nc.sync.dma_start(out=plane[32 * q : 32 * q + 4, :], in_=rows[4 * q : 4 * q + 4, :].bitcast(I32))
+    for r in range(4):
+        nc.sync.dma_start(out=plane[r:P:32, :], in_=rows[r:16:4, :].bitcast(I32))
 
 
 def interleave(copy, grouped, raw, cols):
-    copy(out=grouped[:, cols, :], in_=raw[:, :, cols].rearrange("p j w -> p w j"))
+    copy(
+        out=grouped[:, cols, :].rearrange("p (g i) j -> p g j i", i=4),
+        in_=raw[:, :, cols].rearrange("p j (g i) -> p g j i", i=4),
+    )
 
 
 def quantize(nc, codes, scales, grouped, cols):
@@ -43,6 +47,7 @@ def tile_list_tabgate_silu_kernel(tc, tab_words, tab_scales, w4_words, w4_scales
     nc = tc.nc
     with ExitStack() as ctx:
         keep = ctx.enter_context(tc.tile_pool(name="keep", bufs=1))
+        psum_bias = ctx.enter_context(tc.psum_pool(name="psum_bias", bufs=1))
         psum = ctx.enter_context(tc.psum_pool(name="psum", bufs=4))
 
         offsets = keep.tile([P, S // PER_COL], U16, name="offsets")
@@ -51,6 +56,8 @@ def tile_list_tabgate_silu_kernel(tc, tab_words, tab_scales, w4_words, w4_scales
         w4_w = keep.tile([P, M // 2], I32, name="w4_w", align_bytes=64)
         w4_s = keep.tile([P, M // 4], I32, name="w4_s", align_bytes=64)
         bias = keep.tile([P, M_TILES], F32, name="bias")
+        bias_rows = keep.tile([P, P], F32, name="bias_rows")
+        ident = keep.tile([P, P], F32, name="ident")
         warm = keep.tile([P, 1], F32, name="warm")
         c_raw = [keep.tile([P, PACK, HALF], F32, name="c_raw%d" % h) for h in range(2)]
         u_raw = keep.tile([P, PACK, M], F32, name="u_raw")
@@ -58,12 +65,13 @@ def tile_list_tabgate_silu_kernel(tc, tab_words, tab_scales, w4_words, w4_scales
 
         nc.vector.memset(tab_s[:], 0)
         nc.vector.memset(w4_s[:], 0)
+        nc.gpsimd.memset(bias_rows[:], 0.0)
+        make_identity(nc, ident[:])
 
         c_rows = c.rearrange("(p j) s -> p j s", j=PACK)
         nc.sync.dma_start(offsets[:], offs)
         nc.sync.dma_start(out=tab_w[:], in_=tab_words[0].rearrange("p t i -> p (t i)").bitcast(I32))
-        with nc.allow_non_contiguous_dma(reason="one bias value a partition"):
-            nc.scalar.dma_start(out=bias[:], in_=b.rearrange("(m p) -> p m", p=P))
+        nc.scalar.dma_start(out=bias_rows[:M_TILES, :], in_=b.rearrange("(m p) -> m p", p=P))
         load_scale_rows(nc, tab_s, tab_scales[0])
         nc.sync.dma_start(out=c_raw[0][:], in_=c_rows[:, :, :HALF])
         nc.sync.dma_start(out=c_raw[1][:], in_=c_rows[:, :, HALF:])
@@ -73,7 +81,10 @@ def tile_list_tabgate_silu_kernel(tc, tab_words, tab_scales, w4_words, w4_scales
         for m in range(M_TILES):
             nc.sync.dma_start(out=gates[m][:], in_=gT[m * P : (m + 1) * P, :])
 
-        nc.scalar.activation(out=warm[:], in_=bias[:, 0:1], func=SILU)
+        nc.scalar.activation(out=warm[:], in_=ident[:, 0:1], func=SILU)
+        bias_cols = psum_bias.tile([P, P], F32, name="bias_cols")
+        nc.tensor.transpose(bias_cols[:], bias_rows[:], ident[:])
+        nc.scalar.copy(out=bias[:], in_=bias_cols[:, :M_TILES])
 
         v_codes = keep.tile([P, S], U32, name="v_codes", align_bytes=64)
         v_scales = keep.tile([P, S], U8, name="v_scales", align_bytes=64)
@@ -88,9 +99,9 @@ def tile_list_tabgate_silu_kernel(tc, tab_words, tab_scales, w4_words, w4_scales
         u_scales = keep.tile([P, M], U8, name="u_scales", align_bytes=64)
 
         interleave(nc.scalar.copy, c_bf[0], c_raw[0], slice(0, HALF))
+        interleave(nc.scalar.copy, c_bf[1], c_raw[1], slice(0, 192))
+        interleave(nc.vector.tensor_copy, c_bf[1], c_raw[1], slice(192, HALF))
         quantize(nc, c_codes[0], c_scales[0], c_bf[0], slice(0, HALF))
-        interleave(nc.scalar.copy, c_bf[1], c_raw[1], slice(0, 256))
-        interleave(nc.vector.tensor_copy, c_bf[1], c_raw[1], slice(256, HALF))
         quantize(nc, c_codes[1], c_scales[1], c_bf[1], slice(0, HALF))
         interleave(nc.vector.tensor_copy, u_bf, u_raw, slice(0, P))
         interleave(nc.vector.tensor_copy, u_bf, u_raw, slice(P, 2 * P))

@@ -59,7 +59,7 @@ def tile_list_tabgate_silu_kernel(tc, tab_words, tab_scales, w4_words, w4_scales
         bias_rows = keep.tile([P, P], F32, name="bias_rows")
         ident = keep.tile([P, P], F32, name="ident")
         warm = keep.tile([P, 1], F32, name="warm")
-        c_raw = [keep.tile([P, PACK, HALF], F32, name="c_raw%d" % h) for h in range(2)]
+        c_raw = keep.tile([P, PACK, S], F32, name="c_raw")
         u_raw = keep.tile([P, PACK, M], F32, name="u_raw")
         gates = [keep.tile([P, T], F32, name="gates%d" % m) for m in range(M_TILES)]
 
@@ -68,13 +68,11 @@ def tile_list_tabgate_silu_kernel(tc, tab_words, tab_scales, w4_words, w4_scales
         nc.gpsimd.memset(bias_rows[:], 0.0)
         make_identity(nc, ident[:])
 
-        c_rows = c.rearrange("(p j) s -> p j s", j=PACK)
         nc.sync.dma_start(offsets[:], offs)
         nc.sync.dma_start(out=tab_w[:], in_=tab_words[0].rearrange("p t i -> p (t i)").bitcast(I32))
         nc.scalar.dma_start(out=bias_rows[:M_TILES, :], in_=b.rearrange("(m p) -> m p", p=P))
         load_scale_rows(nc, tab_s, tab_scales[0])
-        nc.sync.dma_start(out=c_raw[0][:], in_=c_rows[:, :, :HALF])
-        nc.sync.dma_start(out=c_raw[1][:], in_=c_rows[:, :, HALF:])
+        nc.sync.dma_start(out=c_raw[:], in_=c.rearrange("(p j) s -> p j s", j=PACK))
         nc.sync.dma_start(out=w4_w[:], in_=w4_words[0].bitcast(I32))
         load_scale_rows(nc, w4_s, w4_scales[0])
         nc.sync.dma_start(out=u_raw[:], in_=u.rearrange("(p j) n -> p j n", j=PACK))
@@ -91,22 +89,22 @@ def tile_list_tabgate_silu_kernel(tc, tab_words, tab_scales, w4_words, w4_scales
         nc.vector.tensor_copy(v_codes[:], tab_w[:].bitcast(U32).indirect(offsets[:]))
         nc.vector.tensor_copy(v_scales[:], tab_s[:].bitcast(U8).indirect(offsets[:]))
 
-        c_bf = [keep.tile([P, HALF, PACK], BF16, name="c_bf%d" % h, align_bytes=64) for h in range(2)]
-        c_codes = [keep.tile([P, HALF], U32, name="c_codes%d" % h, align_bytes=64) for h in range(2)]
-        c_scales = [keep.tile([P, HALF], U8, name="c_scales%d" % h, align_bytes=64) for h in range(2)]
+        c_bf = keep.tile([P, S, PACK], BF16, name="c_bf", align_bytes=64)
+        c_codes = keep.tile([P, S], U32, name="c_codes", align_bytes=64)
+        c_scales = keep.tile([P, S], U8, name="c_scales", align_bytes=64)
         u_bf = keep.tile([P, M, PACK], BF16, name="u_bf", align_bytes=64)
         u_codes = keep.tile([P, M], U32, name="u_codes", align_bytes=64)
         u_scales = keep.tile([P, M], U8, name="u_scales", align_bytes=64)
 
-        interleave(nc.scalar.copy, c_bf[0], c_raw[0], slice(0, HALF))
-        interleave(nc.scalar.copy, c_bf[1], c_raw[1], slice(0, 192))
-        interleave(nc.vector.tensor_copy, c_bf[1], c_raw[1], slice(192, HALF))
-        quantize(nc, c_codes[0], c_scales[0], c_bf[0], slice(0, HALF))
-        quantize(nc, c_codes[1], c_scales[1], c_bf[1], slice(0, HALF))
+        for h in range(2):
+            interleave(nc.scalar.copy, c_bf, c_raw, slice(h * HALF, h * HALF + 192))
+            interleave(nc.vector.tensor_copy, c_bf, c_raw, slice(h * HALF + 192, (h + 1) * HALF))
+        quantize(nc, c_codes, c_scales, c_bf, slice(0, HALF))
         interleave(nc.vector.tensor_copy, u_bf, u_raw, slice(0, P))
         interleave(nc.vector.tensor_copy, u_bf, u_raw, slice(P, 2 * P))
         interleave(nc.scalar.copy, u_bf, u_raw, slice(2 * P, M))
         quantize(nc, u_codes, u_scales, u_bf, slice(0, P))
+        quantize(nc, c_codes, c_scales, c_bf, slice(HALF, S))
         quantize(nc, u_codes, u_scales, u_bf, slice(P, 2 * P))
         quantize(nc, u_codes, u_scales, u_bf, slice(2 * P, M))
 
@@ -132,8 +130,8 @@ def tile_list_tabgate_silu_kernel(tc, tab_words, tab_scales, w4_words, w4_scales
                     out=acc[:],
                     lhsT=u_codes[:, rows].bitcast(FP8X4),
                     lhsT_scale=u_scales[:, rows],
-                    rhs=c_codes[h][:].bitcast(FP8X4),
-                    rhs_scale=c_scales[h][:],
+                    rhs=c_codes[:, cols].bitcast(FP8X4),
+                    rhs_scale=c_scales[:, cols],
                     start=False,
                     stop=True,
                 )

@@ -92,21 +92,29 @@ def tile_list_tabgate_silu_kernel(tc, tab_words, tab_scales, w4_words, w4_scales
         c_bf = keep.tile([P, S, PACK], BF16, name="c_bf", align_bytes=64)
         c_codes = keep.tile([P, S], U32, name="c_codes", align_bytes=64)
         c_scales = keep.tile([P, S], U8, name="c_scales", align_bytes=64)
+        u_bf0 = keep.tile([P, P, PACK], BF16, name="u_bf0", tag="u_bf0", align_bytes=64)
         u_bf = keep.tile([P, M, PACK], BF16, name="u_bf", align_bytes=64)
         u_codes = keep.tile([P, M], U32, name="u_codes", align_bytes=64)
         u_scales = keep.tile([P, M], U8, name="u_scales", align_bytes=64)
 
-        for h in range(2):
-            interleave(nc.scalar.copy, c_bf, c_raw, slice(h * HALF, h * HALF + 192))
-            interleave(nc.vector.tensor_copy, c_bf, c_raw, slice(h * HALF + 192, (h + 1) * HALF))
+        interleave(nc.scalar.copy, c_bf, c_raw, slice(0, 192))
+        interleave(nc.vector.tensor_copy, c_bf, c_raw, slice(192, HALF))
+        interleave(nc.scalar.copy, c_bf, c_raw, slice(HALF, 768))
+        interleave(nc.scalar.copy, c_bf, c_raw, slice(768, 864))
+        interleave(nc.vector.tensor_copy, c_bf, c_raw, slice(864, S))
         quantize(nc, c_codes, c_scales, c_bf, slice(0, HALF))
-        interleave(nc.vector.tensor_copy, u_bf, u_raw, slice(0, P))
+        quantize(nc, c_codes, c_scales, c_bf, slice(HALF, 768))
+        interleave(nc.vector.tensor_copy, u_bf0, u_raw, slice(0, P))
         interleave(nc.vector.tensor_copy, u_bf, u_raw, slice(P, 2 * P))
         interleave(nc.scalar.copy, u_bf, u_raw, slice(2 * P, M))
-        quantize(nc, u_codes, u_scales, u_bf, slice(0, P))
-        quantize(nc, c_codes, c_scales, c_bf, slice(HALF, S))
+        quantize(nc, u_codes, u_scales, u_bf0, slice(0, P))
+        c_tail = keep.tile([P, 256], U32, name="c_tail", tag="u_bf0", align_bytes=64)
+        nc.vector.quantize_mx(
+            out=c_tail[:].bitcast(FP8X4), scales=c_scales[:, 768:], in_=c_bf[:, 768:, :].rearrange("p w j -> p (w j)")
+        )
         quantize(nc, u_codes, u_scales, u_bf, slice(P, 2 * P))
         quantize(nc, u_codes, u_scales, u_bf, slice(2 * P, M))
+        c_runs = (((c_codes[:, :HALF], 0, HALF),), ((c_codes[:, HALF:768], HALF, 768), (c_tail[:], 768, S)))
 
         w4_bytes = w4_w[:].bitcast(U8)
         w4_scale_bytes = w4_s[:].bitcast(U8)
@@ -126,15 +134,16 @@ def tile_list_tabgate_silu_kernel(tc, tab_words, tab_scales, w4_words, w4_scales
                     start=True,
                     stop=False,
                 )
-                nc.tensor.matmul_mx(
-                    out=acc[:],
-                    lhsT=u_codes[:, rows].bitcast(FP8X4),
-                    lhsT_scale=u_scales[:, rows],
-                    rhs=c_codes[:, cols].bitcast(FP8X4),
-                    rhs_scale=c_scales[:, cols],
-                    start=False,
-                    stop=True,
-                )
+                for codes, j0, j1 in c_runs[h]:
+                    nc.tensor.matmul_mx(
+                        out=acc[:, j0 - h * HALF : j1 - h * HALF],
+                        lhsT=u_codes[:, rows].bitcast(FP8X4),
+                        lhsT_scale=u_scales[:, rows],
+                        rhs=codes.bitcast(FP8X4),
+                        rhs_scale=c_scales[:, j0:j1],
+                        start=False,
+                        stop=(j1 % HALF == 0),
+                    )
                 nc.scalar.activation(out=act[:, cols], in_=acc[:], func=SILU, bias=bias[:, m : m + 1])
             j0 = 0
             for width in PIECES[m]:

@@ -22,7 +22,18 @@ PACK = 4
 HALF = 512
 M_TILES = M // P
 PER_COL = 16
-PIECES = ((512, 512), (1024,), (1024,), (512, 256, 256))
+PIECES = ((256, 256, 512), (1024,), (1024,), (512, 256, 256))
+SUMS = ((256, 256, 512), (512, 512), (512, 512), (512, 512))
+QUARTER = 256
+
+
+def runs(start, stop, widths):
+    found = []
+    while start < stop:
+        width = max(w for w in widths if start % w == 0 and start + w <= stop)
+        found.append((start, start + width))
+        start += width
+    return found
 
 
 def load_scale_rows(nc, plane, rows):
@@ -48,7 +59,7 @@ def tile_list_tabgate_silu_kernel(tc, tab_words, tab_scales, w4_words, w4_scales
     with ExitStack() as ctx:
         keep = ctx.enter_context(tc.tile_pool(name="keep", bufs=1))
         psum_bias = ctx.enter_context(tc.psum_pool(name="psum_bias", bufs=1))
-        psum = ctx.enter_context(tc.psum_pool(name="psum", bufs=4))
+        psum = ctx.enter_context(tc.psum_pool(name="psum", bufs=5))
 
         offsets = keep.tile([P, S // PER_COL], U16, name="offsets")
         tab_w = keep.tile([P, T], I32, name="tab_w", align_bytes=64)
@@ -114,7 +125,6 @@ def tile_list_tabgate_silu_kernel(tc, tab_words, tab_scales, w4_words, w4_scales
         )
         quantize(nc, u_codes, u_scales, u_bf, slice(P, 2 * P))
         quantize(nc, u_codes, u_scales, u_bf, slice(2 * P, M))
-        c_runs = (((c_codes[:, :HALF], 0, HALF),), ((c_codes[:, HALF:768], HALF, 768), (c_tail[:], 768, S)))
 
         w4_bytes = w4_w[:].bitcast(U8)
         w4_scale_bytes = w4_s[:].bitcast(U8)
@@ -122,29 +132,32 @@ def tile_list_tabgate_silu_kernel(tc, tab_words, tab_scales, w4_words, w4_scales
             rows = slice(m * P, (m + 1) * P)
             act = keep.tile([P, S], F32, name="act%d" % m)
             res = keep.tile([P, S], F32, name="res%d" % m)
-            for h in range(2):
-                cols = slice(h * HALF, (h + 1) * HALF)
+            s0 = 0
+            for span in SUMS[m]:
+                s1 = s0 + span
                 acc = psum.tile([P, HALF], F32, name="acc")
-                nc.tensor.matmul_mx(
-                    out=acc[:],
-                    lhsT=w4_bytes[:, 2 * m * P : 2 * (m + 1) * P].bitcast(FP4X4),
-                    lhsT_scale=w4_scale_bytes[:, rows],
-                    rhs=v_codes[:, cols].bitcast(FP8X4),
-                    rhs_scale=v_scales[:, cols],
-                    start=True,
-                    stop=False,
-                )
-                for codes, j0, j1 in c_runs[h]:
+                for a0, a1 in runs(s0, s1, (128, 512)):
                     nc.tensor.matmul_mx(
-                        out=acc[:, j0 - h * HALF : j1 - h * HALF],
+                        out=acc[:, a0 - s0 : a1 - s0],
+                        lhsT=w4_bytes[:, 2 * m * P : 2 * (m + 1) * P].bitcast(FP4X4),
+                        lhsT_scale=w4_scale_bytes[:, rows],
+                        rhs=v_codes[:, a0:a1].bitcast(FP8X4),
+                        rhs_scale=v_scales[:, a0:a1],
+                        start=(a0 == s0),
+                        stop=False,
+                    )
+                for a0, a1 in runs(s0, s1, (128, 256, 512) if s0 < HALF else (256,)):
+                    nc.tensor.matmul_mx(
+                        out=acc[:, a0 - s0 : a1 - s0],
                         lhsT=u_codes[:, rows].bitcast(FP8X4),
                         lhsT_scale=u_scales[:, rows],
-                        rhs=codes.bitcast(FP8X4),
-                        rhs_scale=c_scales[:, j0:j1],
+                        rhs=(c_tail[:] if a0 == S - QUARTER else c_codes[:, a0:a1]).bitcast(FP8X4),
+                        rhs_scale=c_scales[:, a0:a1],
                         start=False,
-                        stop=(j1 % HALF == 0),
+                        stop=(a1 == s1),
                     )
-                nc.scalar.activation(out=act[:, cols], in_=acc[:], func=SILU, bias=bias[:, m : m + 1])
+                nc.scalar.activation(out=act[:, s0:s1], in_=acc[:, :span], func=SILU, bias=bias[:, m : m + 1])
+                s0 = s1
             j0 = 0
             for width in PIECES[m]:
                 cols = slice(j0, j0 + width)

@@ -63,7 +63,8 @@ def tile_list_tabgate_silu_kernel(tc, tab_words, tab_scales, w4_words, w4_scales
 
         offsets = keep.tile([P, S // PER_COL], U16, name="offsets")
         tab_w = keep.tile([P, T], I32, name="tab_w", align_bytes=64)
-        tab_s = keep.tile([P, T // 4], I32, name="tab_s", align_bytes=64)
+        tab_s = keep.tile([P, T // 4], I32, name="tab_s", tag="tab_s", align_bytes=64)
+        v_plane = keep.tile([P, S // 4], I32, name="v_plane", align_bytes=64)
         w4_w = keep.tile([P, M // 2], I32, name="w4_w", align_bytes=64)
         w4_s = keep.tile([P, M // 4], I32, name="w4_s", align_bytes=64)
         bias = keep.tile([P, M_TILES], F32, name="bias")
@@ -76,13 +77,14 @@ def tile_list_tabgate_silu_kernel(tc, tab_words, tab_scales, w4_words, w4_scales
 
         nc.vector.memset(tab_s[:], 0)
         nc.vector.memset(w4_s[:], 0)
+        nc.vector.memset(v_plane[:], 0)
         nc.gpsimd.memset(bias_rows[:], 0.0)
         make_identity(nc, ident[:])
 
         nc.sync.dma_start(offsets[:], offs)
         nc.sync.dma_start(out=tab_w[:], in_=tab_words[0].rearrange("p t i -> p (t i)").bitcast(I32))
-        nc.scalar.dma_start(out=bias_rows[:M_TILES, :], in_=b.rearrange("(m p) -> m p", p=P))
-        load_scale_rows(nc, tab_s, tab_scales[0])
+        nc.scalar.dma_start(out=bias_rows[4 : 4 + M_TILES, :], in_=b.rearrange("(m p) -> m p", p=P))
+        nc.sync.dma_start(out=tab_s[4:P:8, :], in_=tab_scales[0].bitcast(I32))
         nc.sync.dma_start(out=c_raw[:], in_=c.rearrange("(p j) s -> p j s", j=PACK))
         nc.sync.dma_start(out=w4_w[:], in_=w4_words[0].bitcast(I32))
         load_scale_rows(nc, w4_s, w4_scales[0])
@@ -93,12 +95,15 @@ def tile_list_tabgate_silu_kernel(tc, tab_words, tab_scales, w4_words, w4_scales
         nc.scalar.activation(out=warm[:], in_=ident[:, 0:1], func=SILU)
         bias_cols = psum_bias.tile([P, P], F32, name="bias_cols")
         nc.tensor.transpose(bias_cols[:], bias_rows[:], ident[:])
-        nc.scalar.copy(out=bias[:], in_=bias_cols[:, :M_TILES])
+        nc.scalar.copy(out=bias[:], in_=bias_cols[:, 4 : 4 + M_TILES])
 
-        v_codes = keep.tile([P, S], U32, name="v_codes", align_bytes=64)
-        v_scales = keep.tile([P, S], U8, name="v_scales", align_bytes=64)
+        s_pick = keep.tile([P, S], U8, name="s_pick", align_bytes=64)
+        nc.vector.tensor_copy(s_pick[:], tab_s[:].bitcast(U8).indirect(offsets[:]))
+        for r in range(4):
+            nc.gpsimd.dma_start(out=v_plane[r:P:32, :], in_=s_pick[4 + 8 * r : P : 32, :].bitcast(I32))
+        v_codes = keep.tile([P, S], U32, name="v_codes", tag="tab_s", align_bytes=64)
         nc.vector.tensor_copy(v_codes[:], tab_w[:].bitcast(U32).indirect(offsets[:]))
-        nc.vector.tensor_copy(v_scales[:], tab_s[:].bitcast(U8).indirect(offsets[:]))
+        v_scales = v_plane[:].bitcast(U8)
 
         c_bf = keep.tile([P, S, PACK], BF16, name="c_bf", align_bytes=64)
         c_codes = keep.tile([P, S], U32, name="c_codes", align_bytes=64)

@@ -58,12 +58,14 @@ def tile_list_tabgate_silu_kernel(tc, tab_words, tab_scales, w4_words, w4_scales
     nc = tc.nc
     with ExitStack() as ctx:
         keep = ctx.enter_context(tc.tile_pool(name="keep", bufs=1))
+        held = ctx.enter_context(tc.tile_pool(name="held", bufs=1))
         psum_bias = ctx.enter_context(tc.psum_pool(name="psum_bias", bufs=1))
         psum = ctx.enter_context(tc.psum_pool(name="psum", bufs=5))
 
         offsets = keep.tile([P, S // PER_COL], U16, name="offsets")
         tab_w = keep.tile([P, T], I32, name="tab_w", align_bytes=64)
-        tab_s = keep.tile([P, T // 4], I32, name="tab_s", tag="tab_s", align_bytes=64)
+        tab_s_all = held.tile([P, 11 * 1024], I32, name="tab_s_all", offset=0, align_bytes=64)
+        tab_s = tab_s_all[:, : T // 4]
         v_plane = keep.tile([P, S // 4], I32, name="v_plane", align_bytes=64)
         w4_w = keep.tile([P, M // 2], I32, name="w4_w", align_bytes=64)
         w4_s = keep.tile([P, M // 4], I32, name="w4_s", align_bytes=64)
@@ -72,10 +74,8 @@ def tile_list_tabgate_silu_kernel(tc, tab_words, tab_scales, w4_words, w4_scales
         ident = keep.tile([P, P], F32, name="ident")
         warm = keep.tile([P, 1], F32, name="warm")
         c_raw = keep.tile([P, PACK, S], F32, name="c_raw")
-        u_raw = keep.tile([P, PACK, M], F32, name="u_raw")
-        gates = [keep.tile([P, T], F32, name="gates%d" % m) for m in range(M_TILES)]
 
-        nc.vector.memset(tab_s[:], 0)
+        nc.vector.memset(tab_s, 0)
         nc.vector.memset(w4_s[:], 0)
         nc.vector.memset(v_plane[:], 0)
         nc.gpsimd.memset(bias_rows[:], 0.0)
@@ -83,14 +83,11 @@ def tile_list_tabgate_silu_kernel(tc, tab_words, tab_scales, w4_words, w4_scales
 
         nc.sync.dma_start(offsets[:], offs)
         nc.sync.dma_start(out=tab_w[:], in_=tab_words[0].rearrange("p t i -> p (t i)").bitcast(I32))
-        nc.scalar.dma_start(out=bias_rows[4 : 4 + M_TILES, :], in_=b.rearrange("(m p) -> m p", p=P))
-        nc.sync.dma_start(out=tab_s[4:P:8, :], in_=tab_scales[0].bitcast(I32))
+        nc.gpsimd.dma_start(out=bias_rows[4 : 4 + M_TILES, :], in_=b.rearrange("(m p) -> m p", p=P))
+        nc.sync.dma_start(out=tab_s_all[4:P:8, : T // 4], in_=tab_scales[0].bitcast(I32))
+        load_scale_rows(nc, w4_s, w4_scales[0])
         nc.sync.dma_start(out=c_raw[:], in_=c.rearrange("(p j) s -> p j s", j=PACK))
         nc.sync.dma_start(out=w4_w[:], in_=w4_words[0].bitcast(I32))
-        load_scale_rows(nc, w4_s, w4_scales[0])
-        nc.sync.dma_start(out=u_raw[:], in_=u.rearrange("(p j) n -> p j n", j=PACK))
-        for m in range(M_TILES):
-            nc.sync.dma_start(out=gates[m][:], in_=gT[m * P : (m + 1) * P, :])
 
         nc.scalar.activation(out=warm[:], in_=ident[:, 0:1], func=SILU)
         bias_cols = psum_bias.tile([P, P], F32, name="bias_cols")
@@ -98,10 +95,15 @@ def tile_list_tabgate_silu_kernel(tc, tab_words, tab_scales, w4_words, w4_scales
         nc.scalar.copy(out=bias[:], in_=bias_cols[:, 4 : 4 + M_TILES])
 
         s_pick = keep.tile([P, S], U8, name="s_pick", align_bytes=64)
-        nc.vector.tensor_copy(s_pick[:], tab_s[:].bitcast(U8).indirect(offsets[:]))
+        nc.vector.tensor_copy(s_pick[:], tab_s.bitcast(U8).indirect(offsets[:]))
         for r in range(4):
-            nc.gpsimd.dma_start(out=v_plane[r:P:32, :], in_=s_pick[4 + 8 * r : P : 32, :].bitcast(I32))
-        v_codes = keep.tile([P, S], U32, name="v_codes", tag="tab_s", align_bytes=64)
+            nc.sync.dma_start(out=v_plane[r:P:32, :], in_=s_pick[4 + 8 * r : P : 32, :].bitcast(I32))
+        u_raw = held.tile([P, PACK, M], F32, name="u_raw", offset=0, align_bytes=64)
+        gates = [held.tile([P, T], F32, name="gates%d" % m, offset=8192 * (m + 1), align_bytes=64) for m in range(M_TILES)]
+        nc.sync.dma_start(out=u_raw[:], in_=u.rearrange("(p j) n -> p j n", j=PACK))
+        for m in range(M_TILES):
+            nc.sync.dma_start(out=gates[m][:], in_=gT[m * P : (m + 1) * P, :])
+        v_codes = held.tile([P, S], U32, name="v_codes", offset=8192 * 5, align_bytes=64)
         nc.vector.tensor_copy(v_codes[:], tab_w[:].bitcast(U32).indirect(offsets[:]))
         v_scales = v_plane[:].bitcast(U8)
 

@@ -81,8 +81,8 @@ def tile_list_tabgate_silu_kernel(tc, tab_words, tab_scales, w4_words, w4_scales
         nc.gpsimd.memset(bias_rows[:], 0.0)
         make_identity(nc, ident[:])
 
-        nc.sync.dma_start(offsets[:], offs)
         nc.sync.dma_start(out=tab_w[:], in_=tab_words[0].rearrange("p t i -> p (t i)").bitcast(I32))
+        nc.sync.dma_start(offsets[:], offs)
         nc.gpsimd.dma_start(out=bias_rows[4 : 4 + M_TILES, :], in_=b.rearrange("(m p) -> m p", p=P))
         nc.sync.dma_start(out=tab_s_all[4:P:8, : T // 4], in_=tab_scales[0].bitcast(I32))
         load_scale_rows(nc, w4_s, w4_scales[0])

@@ -110,7 +110,7 @@ def tile_list_tabgate_silu_kernel(tc, tab_words, tab_scales, w4_words, w4_scales
         c_bf = keep.tile([P, S, PACK], BF16, name="c_bf", align_bytes=64)
         c_codes = keep.tile([P, S], U32, name="c_codes", align_bytes=64)
         c_scales = keep.tile([P, S], U8, name="c_scales", align_bytes=64)
-        u_bf0 = keep.tile([P, P, PACK], BF16, name="u_bf0", tag="u_bf0", align_bytes=64)
+        u_bf0 = held.tile([P, 2 * P, PACK], BF16, name="u_bf0", offset=45056, align_bytes=64)
         u_bf = keep.tile([P, M, PACK], BF16, name="u_bf", align_bytes=64)
         u_codes = keep.tile([P, M], U32, name="u_codes", align_bytes=64)
         u_scales = keep.tile([P, M], U8, name="u_scales", align_bytes=64)
@@ -123,14 +123,15 @@ def tile_list_tabgate_silu_kernel(tc, tab_words, tab_scales, w4_words, w4_scales
         quantize(nc, c_codes, c_scales, c_bf, slice(0, HALF))
         quantize(nc, c_codes, c_scales, c_bf, slice(HALF, 768))
         interleave(nc.vector.tensor_copy, u_bf0, u_raw, slice(0, P))
-        interleave(nc.vector.tensor_copy, u_bf, u_raw, slice(P, 2 * P))
         interleave(nc.scalar.copy, u_bf, u_raw, slice(2 * P, M))
         quantize(nc, u_codes, u_scales, u_bf0, slice(0, P))
-        c_tail = keep.tile([P, 256], U32, name="c_tail", tag="u_bf0", align_bytes=64)
+        c_tail = held.tile([P, 256], U32, name="c_tail", offset=45056, align_bytes=64)
+        u_bf1 = held.tile([P, P, PACK], BF16, name="u_bf1", offset=45056 + 1024, align_bytes=64)
+        interleave(nc.vector.tensor_copy, u_bf1, u_raw[:, :, P : 2 * P], slice(0, P))
         nc.vector.quantize_mx(
             out=c_tail[:].bitcast(FP8X4), scales=c_scales[:, 768:], in_=c_bf[:, 768:, :].rearrange("p w j -> p (w j)")
         )
-        quantize(nc, u_codes, u_scales, u_bf, slice(P, 2 * P))
+        quantize(nc, u_codes[:, P : 2 * P], u_scales[:, P : 2 * P], u_bf1, slice(0, P))
         quantize(nc, u_codes, u_scales, u_bf, slice(2 * P, M))
 
         w4_bytes = w4_w[:].bitcast(U8)

@@ -22,7 +22,7 @@ PACK = 4
 HALF = 512
 M_TILES = M // P
 PER_COL = 16
-PIECES = ((256, 256, 512), (1024,), (1024,), (512, 256, 256))
+PIECES = ((512, 512), (1024,), (1024,), (512, 256, 256))
 SUMS = ((256, 256, 512), (512, 512), (512, 512), (512, 512))
 QUARTER = 256
 
@@ -83,10 +83,10 @@ def tile_list_tabgate_silu_kernel(tc, tab_words, tab_scales, w4_words, w4_scales
 
         nc.sync.dma_start(out=tab_w[:], in_=tab_words[0].rearrange("p t i -> p (t i)").bitcast(I32))
         nc.sync.dma_start(offsets[:], offs)
-        nc.gpsimd.dma_start(out=bias_rows[4 : 4 + M_TILES, :], in_=b.rearrange("(m p) -> m p", p=P))
         nc.sync.dma_start(out=tab_s_all[4:P:8, : T // 4], in_=tab_scales[0].bitcast(I32))
         load_scale_rows(nc, w4_s, w4_scales[0])
         nc.sync.dma_start(out=c_raw[:], in_=c.rearrange("(p j) s -> p j s", j=PACK))
+        nc.sync.dma_start(out=bias_rows[4 : 4 + M_TILES, :], in_=b.rearrange("(m p) -> m p", p=P))
         nc.sync.dma_start(out=w4_w[:], in_=w4_words[0].bitcast(I32))
 
         nc.scalar.activation(out=warm[:], in_=ident[:, 0:1], func=SILU)
@@ -136,10 +136,11 @@ def tile_list_tabgate_silu_kernel(tc, tab_words, tab_scales, w4_words, w4_scales
 
         w4_bytes = w4_w[:].bitcast(U8)
         w4_scale_bytes = w4_s[:].bitcast(U8)
+        res01 = keep.tile([P, 2 * S], F32, name="res01")
         for m in range(M_TILES):
             rows = slice(m * P, (m + 1) * P)
             act = keep.tile([P, S], F32, name="act%d" % m)
-            res = keep.tile([P, S], F32, name="res%d" % m)
+            res = res01[:, m * S : (m + 1) * S] if m < 2 else keep.tile([P, S], F32, name="res%d" % m)
             s0 = 0
             for span in SUMS[m]:
                 s1 = s0 + span
@@ -174,5 +175,9 @@ def tile_list_tabgate_silu_kernel(tc, tab_words, tab_scales, w4_words, w4_scales
                 if m == M_TILES - 1:
                     nc.sync.dma_start(out=out[rows, cols], in_=res[:, cols])
                 j0 += width
-            if m < M_TILES - 1:
+            if m == 1:
+                nc.sync.dma_start(
+                    out=out[: 2 * P, :].rearrange("(m p) s -> p m s", p=P), in_=res01[:].rearrange("p (m s) -> p m s", m=2)
+                )
+            if m == 2:
                 nc.sync.dma_start(out=out[rows, :], in_=res[:])

@@ -1,7 +1,6 @@
 from contextlib import ExitStack
 
 import concourse.mybir as mybir
-from concourse.masks import make_identity
 
 K, M, T, S = 512, 512, 2048, 1024
 FLOPS = 2 * 2 * K * M * S
@@ -59,7 +58,6 @@ def tile_list_tabgate_silu_kernel(tc, tab_words, tab_scales, w4_words, w4_scales
     with ExitStack() as ctx:
         keep = ctx.enter_context(tc.tile_pool(name="keep", bufs=1))
         held = ctx.enter_context(tc.tile_pool(name="held", bufs=1))
-        psum_bias = ctx.enter_context(tc.psum_pool(name="psum_bias", bufs=1))
         psum = ctx.enter_context(tc.psum_pool(name="psum", bufs=5))
 
         offsets = keep.tile([P, S // PER_COL], U16, name="offsets")
@@ -69,30 +67,28 @@ def tile_list_tabgate_silu_kernel(tc, tab_words, tab_scales, w4_words, w4_scales
         v_plane = keep.tile([P, S // 4], I32, name="v_plane", align_bytes=64)
         w4_w = keep.tile([P, M // 2], I32, name="w4_w", align_bytes=64)
         w4_s = keep.tile([P, M // 4], I32, name="w4_s", align_bytes=64)
-        bias = keep.tile([P, M_TILES], F32, name="bias")
-        bias_rows = keep.tile([P, P], F32, name="bias_rows")
-        ident = keep.tile([P, P], F32, name="ident")
+        bias = keep.tile([P, P], F32, name="bias", align_bytes=64)
+        bias_rows = keep.tile([P, P], F32, name="bias_rows", align_bytes=64)
         warm = keep.tile([P, 1], F32, name="warm")
         c_raw = keep.tile([P, PACK, S], F32, name="c_raw")
 
         nc.vector.memset(tab_s, 0)
         nc.vector.memset(w4_s[:], 0)
         nc.vector.memset(v_plane[:], 0)
-        nc.gpsimd.memset(bias_rows[:], 0.0)
-        make_identity(nc, ident[:])
+        nc.vector.memset(bias_rows[:], 0.0)
+        nc.scalar.activation(out=warm[:], in_=bias_rows[:, 0:1], func=SILU)
 
         nc.sync.dma_start(out=tab_w[:], in_=tab_words[0].rearrange("p t i -> p (t i)").bitcast(I32))
         nc.sync.dma_start(offsets[:], offs)
         nc.sync.dma_start(out=tab_s_all[4:P:8, : T // 4], in_=tab_scales[0].bitcast(I32))
         load_scale_rows(nc, w4_s, w4_scales[0])
         nc.sync.dma_start(out=c_raw[:], in_=c.rearrange("(p j) s -> p j s", j=PACK))
-        nc.sync.dma_start(out=bias_rows[4 : 4 + M_TILES, :], in_=b.rearrange("(m p) -> m p", p=P))
+        nc.sync.dma_start(
+            out=bias_rows[4:P:32, :].rearrange("q (m f) -> q m f", f=32), in_=b.rearrange("(m q f) -> q m f", q=4, f=32)
+        )
         nc.sync.dma_start(out=w4_w[:], in_=w4_words[0].bitcast(I32))
 
-        nc.scalar.activation(out=warm[:], in_=ident[:, 0:1], func=SILU)
-        bias_cols = psum_bias.tile([P, P], F32, name="bias_cols")
-        nc.tensor.transpose(bias_cols[:], bias_rows[:], ident[:])
-        nc.scalar.copy(out=bias[:], in_=bias_cols[:, 4 : 4 + M_TILES])
+        nc.vector.transpose(bias[:], bias_rows[:])
 
         s_pick = keep.tile([P, S], U8, name="s_pick", align_bytes=64)
         nc.vector.tensor_copy(s_pick[:], tab_s.bitcast(U8).indirect(offsets[:]))
@@ -165,7 +161,7 @@ def tile_list_tabgate_silu_kernel(tc, tab_words, tab_scales, w4_words, w4_scales
                         start=False,
                         stop=(a1 == s1),
                     )
-                nc.scalar.activation(out=act[:, s0:s1], in_=acc[:, :span], func=SILU, bias=bias[:, m : m + 1])
+                nc.scalar.activation(out=act[:, s0:s1], in_=acc[:, :span], func=SILU, bias=bias[:, 32 * m + 4 : 32 * m + 5])
                 s0 = s1
             j0 = 0
             for width in PIECES[m]:

@@ -60,17 +60,17 @@ def tile_list_tabgate_silu_kernel(tc, tab_words, tab_scales, w4_words, w4_scales
         held = ctx.enter_context(tc.tile_pool(name="held", bufs=1))
         psum = ctx.enter_context(tc.psum_pool(name="psum", bufs=5))
 
-        offsets = keep.tile([P, S // PER_COL], U16, name="offsets")
-        tab_w = keep.tile([P, T], I32, name="tab_w", align_bytes=64)
-        tab_s_all = held.tile([P, 11 * 1024], I32, name="tab_s_all", offset=0, align_bytes=64)
+        offsets = keep.tile([P, S // PER_COL], U16, name="offsets", align_bytes=256)
+        tab_w = keep.tile([P, T], I32, name="tab_w", align_bytes=256)
+        tab_s_all = held.tile([P, 11 * 1024], I32, name="tab_s_all", offset=0, align_bytes=256)
         tab_s = tab_s_all[:, : T // 4]
-        v_plane = keep.tile([P, S // 4], I32, name="v_plane", align_bytes=64)
-        w4_w = keep.tile([P, M // 2], I32, name="w4_w", align_bytes=64)
-        w4_s = keep.tile([P, M // 4], I32, name="w4_s", align_bytes=64)
-        bias = keep.tile([P, P], F32, name="bias", align_bytes=64)
-        bias_rows = keep.tile([P, P], F32, name="bias_rows", align_bytes=64)
+        v_plane = keep.tile([P, S // 4], I32, name="v_plane", align_bytes=256)
+        w4_w = keep.tile([P, M // 2], I32, name="w4_w", align_bytes=256)
+        w4_s = keep.tile([P, M // 4], I32, name="w4_s", align_bytes=256)
+        bias = keep.tile([P, P], F32, name="bias", align_bytes=256)
+        bias_rows = keep.tile([P, P], F32, name="bias_rows", align_bytes=256)
         warm = keep.tile([P, 1], F32, name="warm")
-        c_raw = keep.tile([P, PACK, S], F32, name="c_raw")
+        c_raw = keep.tile([P, PACK, S], F32, name="c_raw", align_bytes=256)
 
         nc.vector.memset(tab_s, 0)
         nc.vector.memset(w4_s[:], 0)
@@ -90,26 +90,26 @@ def tile_list_tabgate_silu_kernel(tc, tab_words, tab_scales, w4_words, w4_scales
 
         nc.vector.transpose(bias[:], bias_rows[:])
 
-        s_pick = keep.tile([P, S], U8, name="s_pick", align_bytes=64)
+        s_pick = keep.tile([P, S], U8, name="s_pick", align_bytes=256)
         nc.vector.tensor_copy(s_pick[:], tab_s.bitcast(U8).indirect(offsets[:]))
         for r in range(4):
             nc.sync.dma_start(out=v_plane[r:P:32, :], in_=s_pick[4 + 8 * r : P : 32, :].bitcast(I32))
-        u_raw = held.tile([P, PACK, M], F32, name="u_raw", offset=0, align_bytes=64)
-        gates = [held.tile([P, T], F32, name="gates%d" % m, offset=8192 * (m + 1), align_bytes=64) for m in range(M_TILES)]
+        u_raw = held.tile([P, PACK, M], F32, name="u_raw", offset=0, align_bytes=256)
+        gates = [held.tile([P, T], F32, name="gates%d" % m, offset=8192 * (m + 1), align_bytes=256) for m in range(M_TILES)]
         nc.sync.dma_start(out=u_raw[:], in_=u.rearrange("(p j) n -> p j n", j=PACK))
         for m in range(M_TILES):
             nc.sync.dma_start(out=gates[m][:], in_=gT[m * P : (m + 1) * P, :])
-        v_codes = held.tile([P, S], U32, name="v_codes", offset=8192 * 5, align_bytes=64)
+        v_codes = held.tile([P, S], U32, name="v_codes", offset=8192 * 5, align_bytes=256)
         nc.vector.tensor_copy(v_codes[:], tab_w[:].bitcast(U32).indirect(offsets[:]))
         v_scales = v_plane[:].bitcast(U8)
 
-        c_bf = keep.tile([P, S, PACK], BF16, name="c_bf", align_bytes=64)
-        c_codes = keep.tile([P, S], U32, name="c_codes", align_bytes=64)
-        c_scales = keep.tile([P, S], U8, name="c_scales", align_bytes=64)
-        u_bf0 = held.tile([P, 2 * P, PACK], BF16, name="u_bf0", offset=45056, align_bytes=64)
-        u_bf = keep.tile([P, M, PACK], BF16, name="u_bf", align_bytes=64)
-        u_codes = keep.tile([P, M], U32, name="u_codes", align_bytes=64)
-        u_scales = keep.tile([P, M], U8, name="u_scales", align_bytes=64)
+        c_bf = keep.tile([P, S, PACK], BF16, name="c_bf", align_bytes=256)
+        c_codes = keep.tile([P, S], U32, name="c_codes", align_bytes=256)
+        c_scales = keep.tile([P, S], U8, name="c_scales", align_bytes=256)
+        u_bf0 = held.tile([P, 2 * P, PACK], BF16, name="u_bf0", offset=45056, align_bytes=256)
+        u_bf = keep.tile([P, M, PACK], BF16, name="u_bf", align_bytes=256)
+        u_codes = keep.tile([P, M], U32, name="u_codes", align_bytes=256)
+        u_scales = keep.tile([P, M], U8, name="u_scales", align_bytes=256)
 
         interleave(nc.scalar.copy, c_bf, c_raw, slice(0, 192))
         interleave(nc.vector.tensor_copy, c_bf, c_raw, slice(192, HALF))
@@ -121,8 +121,8 @@ def tile_list_tabgate_silu_kernel(tc, tab_words, tab_scales, w4_words, w4_scales
         interleave(nc.vector.tensor_copy, u_bf0, u_raw, slice(0, P))
         interleave(nc.scalar.copy, u_bf, u_raw, slice(2 * P, M))
         quantize(nc, u_codes, u_scales, u_bf0, slice(0, P))
-        c_tail = held.tile([P, 256], U32, name="c_tail", offset=45056, align_bytes=64)
-        u_bf1 = held.tile([P, P, PACK], BF16, name="u_bf1", offset=45056 + 1024, align_bytes=64)
+        c_tail = held.tile([P, 256], U32, name="c_tail", offset=45056, align_bytes=256)
+        u_bf1 = held.tile([P, P, PACK], BF16, name="u_bf1", offset=45056 + 1024, align_bytes=256)
         interleave(nc.vector.tensor_copy, u_bf1, u_raw[:, :, P : 2 * P], slice(0, P))
         nc.vector.quantize_mx(
             out=c_tail[:].bitcast(FP8X4), scales=c_scales[:, 768:], in_=c_bf[:, 768:, :].rearrange("p w j -> p (w j)")
@@ -132,11 +132,11 @@ def tile_list_tabgate_silu_kernel(tc, tab_words, tab_scales, w4_words, w4_scales
 
         w4_bytes = w4_w[:].bitcast(U8)
         w4_scale_bytes = w4_s[:].bitcast(U8)
-        res01 = keep.tile([P, 2 * S], F32, name="res01")
+        res01 = keep.tile([P, 2 * S], F32, name="res01", align_bytes=256)
         for m in range(M_TILES):
             rows = slice(m * P, (m + 1) * P)
-            act = keep.tile([P, S], F32, name="act%d" % m)
-            res = res01[:, m * S : (m + 1) * S] if m < 2 else keep.tile([P, S], F32, name="res%d" % m)
+            act = keep.tile([P, S], F32, name="act%d" % m, align_bytes=256)
+            res = res01[:, m * S : (m + 1) * S] if m < 2 else keep.tile([P, S], F32, name="res%d" % m, align_bytes=256)
             s0 = 0
             for span in SUMS[m]:
                 s1 = s0 + span

@@ -21,9 +21,10 @@ PACK = 4
 HALF = 512
 M_TILES = M // P
 PER_COL = 16
-PIECES = ((512, 512), (1024,), (1024,), (512, 256, 256))
+PIECES = ((256, 256, 512), (1024,), (1024,), (512, 256, 256))
 SUMS = ((256, 256, 512), (512, 512), (512, 512), (512, 512))
 QUARTER = 256
+LIVE = 112
 
 
 def runs(start, stop, widths):
@@ -35,8 +36,8 @@ def runs(start, stop, widths):
     return found
 
 
-def load_scale_rows(nc, plane, rows):
-    for r in range(4):
+def load_scale_rows(nc, plane, rows, which):
+    for r in which:
         nc.sync.dma_start(out=plane[r:P:32, :], in_=rows[r:16:4, :].bitcast(I32))
 
 
@@ -69,31 +70,33 @@ def tile_list_tabgate_silu_kernel(tc, tab_words, tab_scales, w4_words, w4_scales
         w4_s = keep.tile([P, M // 4], I32, name="w4_s", align_bytes=256)
         bias = keep.tile([P, P], F32, name="bias", align_bytes=256)
         bias_rows = keep.tile([P, P], F32, name="bias_rows", align_bytes=256)
-        warm = keep.tile([P, 1], F32, name="warm")
+        warm = keep.tile([P, 16], F32, name="warm")
         c_raw = keep.tile([P, PACK, S], F32, name="c_raw", align_bytes=256)
 
-        nc.vector.memset(tab_s, 0)
+        nc.vector.memset(warm[:, 0:1], 0.0)
+        nc.scalar.activation(out=warm[:, 8:9], in_=warm[:, 0:1], func=SILU)
         nc.vector.memset(w4_s[:], 0)
-        nc.vector.memset(v_plane[:], 0)
         nc.vector.memset(bias_rows[:], 0.0)
-        nc.scalar.activation(out=warm[:], in_=bias_rows[:, 0:1], func=SILU)
+        nc.vector.memset(tab_s_all[:LIVE, : T // 4], 0)
+        nc.vector.memset(v_plane[:], 0)
 
-        nc.sync.dma_start(out=tab_w[:], in_=tab_words[0].rearrange("p t i -> p (t i)").bitcast(I32))
+        nc.sync.dma_start(out=w4_w[:], in_=w4_words[0].bitcast(I32))
         nc.sync.dma_start(offsets[:], offs)
-        nc.sync.dma_start(out=tab_s_all[4:P:8, : T // 4], in_=tab_scales[0].bitcast(I32))
-        load_scale_rows(nc, w4_s, w4_scales[0])
-        nc.sync.dma_start(out=c_raw[:], in_=c.rearrange("(p j) s -> p j s", j=PACK))
+        nc.sync.dma_start(out=tab_s_all[LIVE:, : T // 4], in_=tab_scales[0].bitcast(I32))
+        nc.sync.dma_start(out=tab_w[:], in_=tab_words[0].rearrange("p t i -> p (t i)").bitcast(I32))
+        load_scale_rows(nc, w4_s, w4_scales[0], range(2))
         nc.sync.dma_start(
             out=bias_rows[4:P:32, :].rearrange("q (m f) -> q m f", f=32), in_=b.rearrange("(m q f) -> q m f", q=4, f=32)
         )
-        nc.sync.dma_start(out=w4_w[:], in_=w4_words[0].bitcast(I32))
+        nc.sync.dma_start(out=c_raw[:], in_=c.rearrange("(p j) s -> p j s", j=PACK))
+        load_scale_rows(nc, w4_s, w4_scales[0], range(2, 4))
 
         nc.vector.transpose(bias[:], bias_rows[:])
 
         s_pick = keep.tile([P, S], U8, name="s_pick", align_bytes=256)
         nc.vector.tensor_copy(s_pick[:], tab_s.bitcast(U8).indirect(offsets[:]))
         for r in range(4):
-            nc.sync.dma_start(out=v_plane[r:P:32, :], in_=s_pick[4 + 8 * r : P : 32, :].bitcast(I32))
+            nc.sync.dma_start(out=v_plane[r:P:32, :], in_=s_pick[LIVE + r : P : 4, :].bitcast(I32))
         u_raw = held.tile([P, PACK, M], F32, name="u_raw", offset=0, align_bytes=256)
         gates = [held.tile([P, T], F32, name="gates%d" % m, offset=8192 * (m + 1), align_bytes=256) for m in range(M_TILES)]
         nc.sync.dma_start(out=u_raw[:], in_=u.rearrange("(p j) n -> p j n", j=PACK))
@@ -111,11 +114,11 @@ def tile_list_tabgate_silu_kernel(tc, tab_words, tab_scales, w4_words, w4_scales
         u_codes = keep.tile([P, M], U32, name="u_codes", align_bytes=256)
         u_scales = keep.tile([P, M], U8, name="u_scales", align_bytes=256)
 
-        interleave(nc.scalar.copy, c_bf, c_raw, slice(0, 192))
-        interleave(nc.vector.tensor_copy, c_bf, c_raw, slice(192, HALF))
+        interleave(nc.scalar.copy, c_bf, c_raw, slice(0, 128))
+        interleave(nc.vector.tensor_copy, c_bf, c_raw, slice(128, HALF))
         interleave(nc.scalar.copy, c_bf, c_raw, slice(HALF, 768))
-        interleave(nc.scalar.copy, c_bf, c_raw, slice(768, 864))
-        interleave(nc.vector.tensor_copy, c_bf, c_raw, slice(864, S))
+        interleave(nc.scalar.copy, c_bf, c_raw, slice(768, 832))
+        interleave(nc.vector.tensor_copy, c_bf, c_raw, slice(832, S))
         quantize(nc, c_codes, c_scales, c_bf, slice(0, HALF))
         quantize(nc, c_codes, c_scales, c_bf, slice(HALF, 768))
         interleave(nc.vector.tensor_copy, u_bf0, u_raw, slice(0, P))

@@ -18,13 +18,28 @@ MULT = mybir.AluOpType.mult
 
 P = 128
 PACK = 4
+QUADRANT = 32
+BLOCKS = K // 32
 HALF = 512
+QUARTER = 256
+TAIL = S - QUARTER
 M_TILES = M // P
 PER_COL = 16
+ALIGN = 256
+
+SCALE_AT = P - BLOCKS
+BIAS_AT = 4
+
+SUMS = ((128, 128, 256, 512), (512, 512), (512, 512), (512, 512))
 PIECES = ((256, 256, 512), (1024,), (1024,), (512, 256, 256))
-SUMS = ((256, 256, 512), (512, 512), (512, 512), (512, 512))
-QUARTER = 256
-LIVE = 112
+BANKS = len(SUMS[0]) + len(SUMS[1])
+SCALAR_HEAD = 128
+SCALAR_TAIL = 64
+
+ROW_BYTES = 4 * T
+V_CODES_AT = (1 + M_TILES) * ROW_BYTES
+STAGE_AT = V_CODES_AT + 4 * S
+U_TILE_BYTES = 2 * PACK * P
 
 
 def runs(start, stop, widths):
@@ -38,7 +53,7 @@ def runs(start, stop, widths):
 
 def load_scale_rows(nc, plane, rows, which):
     for r in which:
-        nc.sync.dma_start(out=plane[r:P:32, :], in_=rows[r:16:4, :].bitcast(I32))
+        nc.sync.dma_start(out=plane[r:P:QUADRANT, :], in_=rows[r:BLOCKS:4, :].bitcast(I32))
 
 
 def interleave(copy, grouped, raw, cols):
@@ -59,87 +74,88 @@ def tile_list_tabgate_silu_kernel(tc, tab_words, tab_scales, w4_words, w4_scales
     with ExitStack() as ctx:
         keep = ctx.enter_context(tc.tile_pool(name="keep", bufs=1))
         held = ctx.enter_context(tc.tile_pool(name="held", bufs=1))
-        psum = ctx.enter_context(tc.psum_pool(name="psum", bufs=5))
+        psum = ctx.enter_context(tc.psum_pool(name="psum", bufs=BANKS))
 
-        offsets = keep.tile([P, S // PER_COL], U16, name="offsets", align_bytes=256)
-        tab_w = keep.tile([P, T], I32, name="tab_w", align_bytes=256)
-        tab_s_all = held.tile([P, 11 * 1024], I32, name="tab_s_all", offset=0, align_bytes=256)
+        offsets = keep.tile([P, S // PER_COL], U16, name="offsets", align_bytes=ALIGN)
+        tab_w = keep.tile([P, T], I32, name="tab_w", align_bytes=ALIGN)
+        tab_s_all = held.tile([P, STAGE_AT // 4], I32, name="tab_s_all", offset=0, align_bytes=ALIGN)
         tab_s = tab_s_all[:, : T // 4]
-        v_plane = keep.tile([P, S // 4], I32, name="v_plane", align_bytes=256)
-        w4_w = keep.tile([P, M // 2], I32, name="w4_w", align_bytes=256)
-        w4_s = keep.tile([P, M // 4], I32, name="w4_s", align_bytes=256)
-        bias = keep.tile([P, P], F32, name="bias", align_bytes=256)
-        bias_rows = keep.tile([P, P], F32, name="bias_rows", align_bytes=256)
+        v_plane = keep.tile([P, S // 4], I32, name="v_plane", align_bytes=ALIGN)
+        w4_w = keep.tile([P, M // 2], I32, name="w4_w", align_bytes=ALIGN)
+        w4_s = keep.tile([P, M // 4], I32, name="w4_s", align_bytes=ALIGN)
+        bias = keep.tile([P, P], F32, name="bias", align_bytes=ALIGN)
+        bias_rows = keep.tile([P, P], F32, name="bias_rows", align_bytes=ALIGN)
         warm = keep.tile([P, 16], F32, name="warm")
-        c_raw = keep.tile([P, PACK, S], F32, name="c_raw", align_bytes=256)
+        c_raw = keep.tile([P, PACK, S], F32, name="c_raw", align_bytes=ALIGN)
 
         nc.vector.memset(warm[:, 0:1], 0.0)
         nc.scalar.activation(out=warm[:, 8:9], in_=warm[:, 0:1], func=SILU)
         nc.vector.memset(w4_s[:], 0)
         nc.vector.memset(bias_rows[:], 0.0)
-        nc.vector.memset(tab_s_all[:LIVE, : T // 4], 0)
+        nc.vector.memset(tab_s_all[:SCALE_AT, : T // 4], 0)
         nc.vector.memset(v_plane[:], 0)
 
         nc.sync.dma_start(out=w4_w[:], in_=w4_words[0].bitcast(I32))
         nc.sync.dma_start(offsets[:], offs)
-        nc.sync.dma_start(out=tab_s_all[LIVE:, : T // 4], in_=tab_scales[0].bitcast(I32))
+        nc.sync.dma_start(out=tab_s_all[SCALE_AT:, : T // 4], in_=tab_scales[0].bitcast(I32))
         nc.sync.dma_start(out=tab_w[:], in_=tab_words[0].rearrange("p t i -> p (t i)").bitcast(I32))
         load_scale_rows(nc, w4_s, w4_scales[0], range(2))
         nc.sync.dma_start(
-            out=bias_rows[4:P:32, :].rearrange("q (m f) -> q m f", f=32), in_=b.rearrange("(m q f) -> q m f", q=4, f=32)
+            out=bias_rows[BIAS_AT:P:QUADRANT, :].rearrange("q (m f) -> q m f", f=QUADRANT),
+            in_=b.rearrange("(m q f) -> q m f", q=4, f=QUADRANT),
         )
         nc.sync.dma_start(out=c_raw[:], in_=c.rearrange("(p j) s -> p j s", j=PACK))
         load_scale_rows(nc, w4_s, w4_scales[0], range(2, 4))
 
         nc.vector.transpose(bias[:], bias_rows[:])
 
-        s_pick = keep.tile([P, S], U8, name="s_pick", align_bytes=256)
+        s_pick = keep.tile([P, S], U8, name="s_pick", align_bytes=ALIGN)
         nc.vector.tensor_copy(s_pick[:], tab_s.bitcast(U8).indirect(offsets[:]))
         for r in range(4):
-            nc.sync.dma_start(out=v_plane[r:P:32, :], in_=s_pick[LIVE + r : P : 4, :].bitcast(I32))
-        u_raw = held.tile([P, PACK, M], F32, name="u_raw", offset=0, align_bytes=256)
-        gates = [held.tile([P, T], F32, name="gates%d" % m, offset=8192 * (m + 1), align_bytes=256) for m in range(M_TILES)]
+            nc.sync.dma_start(out=v_plane[r:P:QUADRANT, :], in_=s_pick[SCALE_AT + r : P : 4, :].bitcast(I32))
+        u_raw = held.tile([P, PACK, M], F32, name="u_raw", offset=0, align_bytes=ALIGN)
+        gates = [
+            held.tile([P, T], F32, name="gates%d" % m, offset=ROW_BYTES * (m + 1), align_bytes=ALIGN) for m in range(M_TILES)
+        ]
         nc.sync.dma_start(out=u_raw[:], in_=u.rearrange("(p j) n -> p j n", j=PACK))
         for m in range(M_TILES):
             nc.sync.dma_start(out=gates[m][:], in_=gT[m * P : (m + 1) * P, :])
-        v_codes = held.tile([P, S], U32, name="v_codes", offset=8192 * 5, align_bytes=256)
+        v_codes = held.tile([P, S], U32, name="v_codes", offset=V_CODES_AT, align_bytes=ALIGN)
         nc.vector.tensor_copy(v_codes[:], tab_w[:].bitcast(U32).indirect(offsets[:]))
         v_scales = v_plane[:].bitcast(U8)
 
-        c_bf = keep.tile([P, S, PACK], BF16, name="c_bf", align_bytes=256)
-        c_codes = keep.tile([P, S], U32, name="c_codes", align_bytes=256)
-        c_scales = keep.tile([P, S], U8, name="c_scales", align_bytes=256)
-        u_bf0 = held.tile([P, 2 * P, PACK], BF16, name="u_bf0", offset=45056, align_bytes=256)
-        u_bf = keep.tile([P, M, PACK], BF16, name="u_bf", align_bytes=256)
-        u_codes = keep.tile([P, M], U32, name="u_codes", align_bytes=256)
-        u_scales = keep.tile([P, M], U8, name="u_scales", align_bytes=256)
+        c_bf = keep.tile([P, S, PACK], BF16, name="c_bf", align_bytes=ALIGN)
+        c_codes = keep.tile([P, S], U32, name="c_codes", align_bytes=ALIGN)
+        c_scales = keep.tile([P, S], U8, name="c_scales", align_bytes=ALIGN)
+        u_bf0 = held.tile([P, 2 * P, PACK], BF16, name="u_bf0", offset=STAGE_AT, align_bytes=ALIGN)
+        u_bf = keep.tile([P, M, PACK], BF16, name="u_bf", align_bytes=ALIGN)
+        u_codes = keep.tile([P, M], U32, name="u_codes", align_bytes=ALIGN)
+        u_scales = keep.tile([P, M], U8, name="u_scales", align_bytes=ALIGN)
 
-        interleave(nc.scalar.copy, c_bf, c_raw, slice(0, 128))
-        interleave(nc.vector.tensor_copy, c_bf, c_raw, slice(128, HALF))
-        interleave(nc.scalar.copy, c_bf, c_raw, slice(HALF, 768))
-        interleave(nc.scalar.copy, c_bf, c_raw, slice(768, 832))
-        interleave(nc.vector.tensor_copy, c_bf, c_raw, slice(832, S))
+        interleave(nc.scalar.copy, c_bf, c_raw, slice(0, SCALAR_HEAD))
+        interleave(nc.vector.tensor_copy, c_bf, c_raw, slice(SCALAR_HEAD, HALF))
+        interleave(nc.scalar.copy, c_bf, c_raw, slice(HALF, TAIL))
+        interleave(nc.scalar.copy, c_bf, c_raw, slice(TAIL, TAIL + SCALAR_TAIL))
+        interleave(nc.vector.tensor_copy, c_bf, c_raw, slice(TAIL + SCALAR_TAIL, S))
         quantize(nc, c_codes, c_scales, c_bf, slice(0, HALF))
-        quantize(nc, c_codes, c_scales, c_bf, slice(HALF, 768))
+        quantize(nc, c_codes, c_scales, c_bf, slice(HALF, TAIL))
         interleave(nc.vector.tensor_copy, u_bf0, u_raw, slice(0, P))
         interleave(nc.scalar.copy, u_bf, u_raw, slice(2 * P, M))
         quantize(nc, u_codes, u_scales, u_bf0, slice(0, P))
-        c_tail = held.tile([P, 256], U32, name="c_tail", offset=45056, align_bytes=256)
-        u_bf1 = held.tile([P, P, PACK], BF16, name="u_bf1", offset=45056 + 1024, align_bytes=256)
+        c_tail = held.tile([P, QUARTER], U32, name="c_tail", offset=STAGE_AT, align_bytes=ALIGN)
+        u_bf1 = held.tile([P, P, PACK], BF16, name="u_bf1", offset=STAGE_AT + U_TILE_BYTES, align_bytes=ALIGN)
         interleave(nc.vector.tensor_copy, u_bf1, u_raw[:, :, P : 2 * P], slice(0, P))
-        nc.vector.quantize_mx(
-            out=c_tail[:].bitcast(FP8X4), scales=c_scales[:, 768:], in_=c_bf[:, 768:, :].rearrange("p w j -> p (w j)")
-        )
+        quantize(nc, c_tail, c_scales[:, TAIL:], c_bf[:, TAIL:, :], slice(0, QUARTER))
         quantize(nc, u_codes[:, P : 2 * P], u_scales[:, P : 2 * P], u_bf1, slice(0, P))
         quantize(nc, u_codes, u_scales, u_bf, slice(2 * P, M))
 
         w4_bytes = w4_w[:].bitcast(U8)
         w4_scale_bytes = w4_s[:].bitcast(U8)
-        res01 = keep.tile([P, 2 * S], F32, name="res01", align_bytes=256)
+        res01 = keep.tile([P, 2 * S], F32, name="res01", align_bytes=ALIGN)
         for m in range(M_TILES):
             rows = slice(m * P, (m + 1) * P)
-            act = keep.tile([P, S], F32, name="act%d" % m, align_bytes=256)
-            res = res01[:, m * S : (m + 1) * S] if m < 2 else keep.tile([P, S], F32, name="res%d" % m, align_bytes=256)
+            act = keep.tile([P, S], F32, name="act%d" % m, align_bytes=ALIGN)
+            res = res01[:, m * S : (m + 1) * S] if m < 2 else keep.tile([P, S], F32, name="res%d" % m, align_bytes=ALIGN)
             s0 = 0
             for span in SUMS[m]:
                 s1 = s0 + span
@@ -154,17 +170,18 @@ def tile_list_tabgate_silu_kernel(tc, tab_words, tab_scales, w4_words, w4_scales
                         start=(a0 == s0),
                         stop=False,
                     )
-                for a0, a1 in runs(s0, s1, (128, 256, 512) if s0 < HALF else (256,)):
+                for a0, a1 in runs(s0, s1, (128, 256, 512) if s0 < HALF else (QUARTER,)):
                     nc.tensor.matmul_mx(
                         out=acc[:, a0 - s0 : a1 - s0],
                         lhsT=u_codes[:, rows].bitcast(FP8X4),
                         lhsT_scale=u_scales[:, rows],
-                        rhs=(c_tail[:] if a0 == S - QUARTER else c_codes[:, a0:a1]).bitcast(FP8X4),
+                        rhs=(c_tail[:] if a0 == TAIL else c_codes[:, a0:a1]).bitcast(FP8X4),
                         rhs_scale=c_scales[:, a0:a1],
                         start=False,
                         stop=(a1 == s1),
                     )
-                nc.scalar.activation(out=act[:, s0:s1], in_=acc[:, :span], func=SILU, bias=bias[:, 32 * m + 4 : 32 * m + 5])
+                bias_col = QUADRANT * m + BIAS_AT
+                nc.scalar.activation(out=act[:, s0:s1], in_=acc[:, :span], func=SILU, bias=bias[:, bias_col : bias_col + 1])
                 s0 = s1
             j0 = 0
             for width in PIECES[m]:

@@ -35,11 +35,11 @@ PIECES = ((256, 256, 512), (1024,), (1024,), (512, 256, 256))
 BANKS = len(SUMS[0]) + len(SUMS[1])
 SCALAR_HEAD = 128
 SCALAR_TAIL = 64
+U_VECTOR = 96
 
 ROW_BYTES = 4 * T
 V_CODES_AT = (1 + M_TILES) * ROW_BYTES
 STAGE_AT = V_CODES_AT + 4 * S
-U_TILE_BYTES = 2 * PACK * P
 
 
 def runs(start, stop, widths):
@@ -127,7 +127,7 @@ def tile_list_tabgate_silu_kernel(tc, tab_words, tab_scales, w4_words, w4_scales
         c_bf = keep.tile([P, S, PACK], BF16, name="c_bf", align_bytes=ALIGN)
         c_codes = keep.tile([P, S], U32, name="c_codes", align_bytes=ALIGN)
         c_scales = keep.tile([P, S], U8, name="c_scales", align_bytes=ALIGN)
-        u_bf0 = held.tile([P, 2 * P, PACK], BF16, name="u_bf0", offset=STAGE_AT, align_bytes=ALIGN)
+        u_bf0 = held.tile([P, P, PACK], BF16, name="u_bf0", offset=STAGE_AT, align_bytes=ALIGN)
         u_bf = keep.tile([P, M, PACK], BF16, name="u_bf", align_bytes=ALIGN)
         u_codes = keep.tile([P, M], U32, name="u_codes", align_bytes=ALIGN)
         u_scales = keep.tile([P, M], U8, name="u_scales", align_bytes=ALIGN)
@@ -140,14 +140,12 @@ def tile_list_tabgate_silu_kernel(tc, tab_words, tab_scales, w4_words, w4_scales
         quantize(nc, c_codes, c_scales, c_bf, slice(0, HALF))
         quantize(nc, c_codes, c_scales, c_bf, slice(HALF, TAIL))
         interleave(nc.vector.tensor_copy, u_bf0, u_raw, slice(0, P))
-        interleave(nc.scalar.copy, u_bf, u_raw, slice(2 * P, M))
+        interleave(nc.vector.tensor_copy, u_bf, u_raw, slice(P, P + U_VECTOR))
+        interleave(nc.scalar.copy, u_bf, u_raw, slice(P + U_VECTOR, M))
         quantize(nc, u_codes, u_scales, u_bf0, slice(0, P))
         c_tail = held.tile([P, QUARTER], U32, name="c_tail", offset=STAGE_AT, align_bytes=ALIGN)
-        u_bf1 = held.tile([P, P, PACK], BF16, name="u_bf1", offset=STAGE_AT + U_TILE_BYTES, align_bytes=ALIGN)
-        interleave(nc.vector.tensor_copy, u_bf1, u_raw[:, :, P : 2 * P], slice(0, P))
         quantize(nc, c_tail, c_scales[:, TAIL:], c_bf[:, TAIL:, :], slice(0, QUARTER))
-        quantize(nc, u_codes[:, P : 2 * P], u_scales[:, P : 2 * P], u_bf1, slice(0, P))
-        quantize(nc, u_codes, u_scales, u_bf, slice(2 * P, M))
+        quantize(nc, u_codes, u_scales, u_bf, slice(P, M))
 
         w4_bytes = w4_w[:].bitcast(U8)
         w4_scale_bytes = w4_s[:].bitcast(U8)

@@ -51,11 +51,6 @@ def runs(start, stop, widths):
     return found
 
 
-def load_scale_rows(nc, plane, rows, which):
-    for r in which:
-        nc.sync.dma_start(out=plane[r:P:QUADRANT, :], in_=rows[r:BLOCKS:4, :].bitcast(I32))
-
-
 def interleave(copy, grouped, raw, cols):
     copy(
         out=grouped[:, cols, :].rearrange("p (g i) j -> p g j i", i=4),
@@ -88,24 +83,22 @@ def tile_list_tabgate_silu_kernel(tc, tab_words, tab_scales, w4_words, w4_scales
         warm = keep.tile([P, 16], F32, name="warm")
         c_raw = keep.tile([P, PACK, S], F32, name="c_raw", align_bytes=ALIGN)
 
+        for r in range(4):
+            nc.scalar.dma_start(out=w4_s[r:P:QUADRANT, :], in_=w4_scales[0][r:BLOCKS:4, :].bitcast(I32))
         nc.vector.memset(warm[:, 0:1], 0.0)
         nc.scalar.activation(out=warm[:, 8:9], in_=warm[:, 0:1], func=SILU)
-        nc.vector.memset(w4_s[:], 0)
         nc.vector.memset(bias_rows[:], 0.0)
         nc.vector.memset(tab_s_all[:SCALE_AT, : T // 4], 0)
-        nc.vector.memset(v_plane[:], 0)
 
         nc.sync.dma_start(out=w4_w[:], in_=w4_words[0].bitcast(I32))
         nc.sync.dma_start(offsets[:], offs)
         nc.sync.dma_start(out=tab_s_all[SCALE_AT:, : T // 4], in_=tab_scales[0].bitcast(I32))
         nc.sync.dma_start(out=tab_w[:], in_=tab_words[0].rearrange("p t i -> p (t i)").bitcast(I32))
-        load_scale_rows(nc, w4_s, w4_scales[0], range(2))
         nc.sync.dma_start(
             out=bias_rows[BIAS_AT:P:QUADRANT, :].rearrange("q (m f) -> q m f", f=QUADRANT),
             in_=b.rearrange("(m q f) -> q m f", q=4, f=QUADRANT),
         )
         nc.sync.dma_start(out=c_raw[:], in_=c.rearrange("(p j) s -> p j s", j=PACK))
-        load_scale_rows(nc, w4_s, w4_scales[0], range(2, 4))
 
         nc.vector.transpose(bias[:], bias_rows[:])
 

@@ -35,7 +35,7 @@ PIECES = ((256, 256, 512), (1024,), (1024,), (512, 256, 256))
 BANKS = len(SUMS[0]) + len(SUMS[1])
 SCALAR_HEAD = 128
 SCALAR_TAIL = 64
-U_VECTOR = 96
+U_VECTOR = 160
 
 ROW_BYTES = 4 * T
 V_CODES_AT = (1 + M_TILES) * ROW_BYTES

from contextlib import ExitStack

import concourse.mybir as mybir

K, M, T, S = 512, 512, 2048, 1024
FLOPS = 2 * 2 * K * M * S

F32 = mybir.dt.float32
BF16 = mybir.dt.bfloat16
I32 = mybir.dt.int32
U32 = mybir.dt.uint32
U16 = mybir.dt.uint16
U8 = mybir.dt.uint8
FP8X4 = mybir.dt.float8_e4m3fn_x4
FP4X4 = mybir.dt.float4_e2m1fn_x4
SILU = mybir.ActivationFunctionType.Silu
MULT = mybir.AluOpType.mult

P = 128
PACK = 4
QUADRANT = 32
BLOCKS = K // 32
HALF = 512
QUARTER = 256
TAIL = S - QUARTER
M_TILES = M // P
PER_COL = 16
ALIGN = 256

SCALE_AT = P - BLOCKS
BIAS_AT = 4

SUMS = ((128, 128, 256, 512), (512, 512), (512, 512), (512, 512))
PIECES = ((256, 256, 512), (1024,), (1024,), (512, 256, 256))
BANKS = len(SUMS[0]) + len(SUMS[1])
SCALAR_HEAD = 128
SCALAR_TAIL = 64
U_VECTOR = 160

ROW_BYTES = 4 * T
V_CODES_AT = (1 + M_TILES) * ROW_BYTES
STAGE_AT = V_CODES_AT + 4 * S


def runs(start, stop, widths):
    found = []
    while start < stop:
        width = max(w for w in widths if start % w == 0 and start + w <= stop)
        found.append((start, start + width))
        start += width
    return found


def interleave(copy, grouped, raw, cols):
    copy(
        out=grouped[:, cols, :].rearrange("p (g i) j -> p g j i", i=4),
        in_=raw[:, :, cols].rearrange("p j (g i) -> p g j i", i=4),
    )


def quantize(nc, codes, scales, grouped, cols):
    nc.vector.quantize_mx(
        out=codes[:, cols].bitcast(FP8X4), scales=scales[:, cols], in_=grouped[:, cols, :].rearrange("p w j -> p (w j)")
    )


def tile_list_tabgate_silu_kernel(tc, tab_words, tab_scales, w4_words, w4_scales, c, u, gT, b, offs, out):
    nc = tc.nc
    with ExitStack() as ctx:
        keep = ctx.enter_context(tc.tile_pool(name="keep", bufs=1))
        held = ctx.enter_context(tc.tile_pool(name="held", bufs=1))
        psum = ctx.enter_context(tc.psum_pool(name="psum", bufs=BANKS))

        offsets = keep.tile([P, S // PER_COL], U16, name="offsets", align_bytes=ALIGN)
        tab_w = keep.tile([P, T], I32, name="tab_w", align_bytes=ALIGN)
        tab_s_all = held.tile([P, STAGE_AT // 4], I32, name="tab_s_all", offset=0, align_bytes=ALIGN)
        tab_s = tab_s_all[:, : T // 4]
        v_plane = keep.tile([P, S // 4], I32, name="v_plane", align_bytes=ALIGN)
        w4_w = keep.tile([P, M // 2], I32, name="w4_w", align_bytes=ALIGN)
        w4_s = keep.tile([P, M // 4], I32, name="w4_s", align_bytes=ALIGN)
        bias = keep.tile([P, P], F32, name="bias", align_bytes=ALIGN)
        bias_rows = keep.tile([P, P], F32, name="bias_rows", align_bytes=ALIGN)
        warm = keep.tile([P, 16], F32, name="warm")
        c_raw = keep.tile([P, PACK, S], F32, name="c_raw", align_bytes=ALIGN)

        for r in range(4):
            nc.scalar.dma_start(out=w4_s[r:P:QUADRANT, :], in_=w4_scales[0][r:BLOCKS:4, :].bitcast(I32))
        nc.vector.memset(warm[:, 0:1], 0.0)
        nc.scalar.activation(out=warm[:, 8:9], in_=warm[:, 0:1], func=SILU)
        nc.vector.memset(bias_rows[:], 0.0)
        nc.vector.memset(tab_s_all[:SCALE_AT, : T // 4], 0)

        nc.sync.dma_start(out=w4_w[:], in_=w4_words[0].bitcast(I32))
        nc.sync.dma_start(offsets[:], offs)
        nc.sync.dma_start(out=tab_s_all[SCALE_AT:, : T // 4], in_=tab_scales[0].bitcast(I32))
        nc.sync.dma_start(out=tab_w[:], in_=tab_words[0].rearrange("p t i -> p (t i)").bitcast(I32))
        nc.sync.dma_start(
            out=bias_rows[BIAS_AT:P:QUADRANT, :].rearrange("q (m f) -> q m f", f=QUADRANT),
            in_=b.rearrange("(m q f) -> q m f", q=4, f=QUADRANT),
        )
        nc.sync.dma_start(out=c_raw[:], in_=c.rearrange("(p j) s -> p j s", j=PACK))

        nc.vector.transpose(bias[:], bias_rows[:])

        s_pick = keep.tile([P, S], U8, name="s_pick", align_bytes=ALIGN)
        nc.vector.tensor_copy(s_pick[:], tab_s.bitcast(U8).indirect(offsets[:]))
        for r in range(4):
            nc.sync.dma_start(out=v_plane[r:P:QUADRANT, :], in_=s_pick[SCALE_AT + r : P : 4, :].bitcast(I32))
        u_raw = held.tile([P, PACK, M], F32, name="u_raw", offset=0, align_bytes=ALIGN)
        gates = [
            held.tile([P, T], F32, name="gates%d" % m, offset=ROW_BYTES * (m + 1), align_bytes=ALIGN) for m in range(M_TILES)
        ]
        nc.sync.dma_start(out=u_raw[:], in_=u.rearrange("(p j) n -> p j n", j=PACK))
        for m in range(M_TILES):
            nc.sync.dma_start(out=gates[m][:], in_=gT[m * P : (m + 1) * P, :])
        v_codes = held.tile([P, S], U32, name="v_codes", offset=V_CODES_AT, align_bytes=ALIGN)
        nc.vector.tensor_copy(v_codes[:], tab_w[:].bitcast(U32).indirect(offsets[:]))
        v_scales = v_plane[:].bitcast(U8)

        c_bf = keep.tile([P, S, PACK], BF16, name="c_bf", align_bytes=ALIGN)
        c_codes = keep.tile([P, S], U32, name="c_codes", align_bytes=ALIGN)
        c_scales = keep.tile([P, S], U8, name="c_scales", align_bytes=ALIGN)
        u_bf0 = held.tile([P, P, PACK], BF16, name="u_bf0", offset=STAGE_AT, align_bytes=ALIGN)
        u_bf = keep.tile([P, M, PACK], BF16, name="u_bf", align_bytes=ALIGN)
        u_codes = keep.tile([P, M], U32, name="u_codes", align_bytes=ALIGN)
        u_scales = keep.tile([P, M], U8, name="u_scales", align_bytes=ALIGN)

        interleave(nc.scalar.copy, c_bf, c_raw, slice(0, SCALAR_HEAD))
        interleave(nc.vector.tensor_copy, c_bf, c_raw, slice(SCALAR_HEAD, HALF))
        interleave(nc.scalar.copy, c_bf, c_raw, slice(HALF, TAIL))
        interleave(nc.scalar.copy, c_bf, c_raw, slice(TAIL, TAIL + SCALAR_TAIL))
        interleave(nc.vector.tensor_copy, c_bf, c_raw, slice(TAIL + SCALAR_TAIL, S))
        quantize(nc, c_codes, c_scales, c_bf, slice(0, HALF))
        quantize(nc, c_codes, c_scales, c_bf, slice(HALF, TAIL))
        interleave(nc.vector.tensor_copy, u_bf0, u_raw, slice(0, P))
        interleave(nc.vector.tensor_copy, u_bf, u_raw, slice(P, P + U_VECTOR))
        interleave(nc.scalar.copy, u_bf, u_raw, slice(P + U_VECTOR, M))
        quantize(nc, u_codes, u_scales, u_bf0, slice(0, P))
        c_tail = held.tile([P, QUARTER], U32, name="c_tail", offset=STAGE_AT, align_bytes=ALIGN)
        quantize(nc, c_tail, c_scales[:, TAIL:], c_bf[:, TAIL:, :], slice(0, QUARTER))
        quantize(nc, u_codes, u_scales, u_bf, slice(P, M))

        w4_bytes = w4_w[:].bitcast(U8)
        w4_scale_bytes = w4_s[:].bitcast(U8)
        res01 = keep.tile([P, 2 * S], F32, name="res01", align_bytes=ALIGN)
        for m in range(M_TILES):
            rows = slice(m * P, (m + 1) * P)
            act = keep.tile([P, S], F32, name="act%d" % m, align_bytes=ALIGN)
            res = res01[:, m * S : (m + 1) * S] if m < 2 else keep.tile([P, S], F32, name="res%d" % m, align_bytes=ALIGN)
            s0 = 0
            for span in SUMS[m]:
                s1 = s0 + span
                acc = psum.tile([P, HALF], F32, name="acc")
                for a0, a1 in runs(s0, s1, (128, 512)):
                    nc.tensor.matmul_mx(
                        out=acc[:, a0 - s0 : a1 - s0],
                        lhsT=w4_bytes[:, 2 * m * P : 2 * (m + 1) * P].bitcast(FP4X4),
                        lhsT_scale=w4_scale_bytes[:, rows],
                        rhs=v_codes[:, a0:a1].bitcast(FP8X4),
                        rhs_scale=v_scales[:, a0:a1],
                        start=(a0 == s0),
                        stop=False,
                    )
                for a0, a1 in runs(s0, s1, (128, 256, 512) if s0 < HALF else (QUARTER,)):
                    nc.tensor.matmul_mx(
                        out=acc[:, a0 - s0 : a1 - s0],
                        lhsT=u_codes[:, rows].bitcast(FP8X4),
                        lhsT_scale=u_scales[:, rows],
                        rhs=(c_tail[:] if a0 == TAIL else c_codes[:, a0:a1]).bitcast(FP8X4),
                        rhs_scale=c_scales[:, a0:a1],
                        start=False,
                        stop=(a1 == s1),
                    )
                bias_col = QUADRANT * m + BIAS_AT
                nc.scalar.activation(out=act[:, s0:s1], in_=acc[:, :span], func=SILU, bias=bias[:, bias_col : bias_col + 1])
                s0 = s1
            j0 = 0
            for width in PIECES[m]:
                cols = slice(j0, j0 + width)
                picked = gates[m][:].indirect(offsets[:, j0 // PER_COL : (j0 + width) // PER_COL])
                nc.vector.tensor_tensor(res[:, cols], picked, act[:, cols], MULT)
                if m == M_TILES - 1:
                    nc.sync.dma_start(out=out[rows, cols], in_=res[:, cols])
                j0 += width
            if m == 1:
                nc.sync.dma_start(
                    out=out[: 2 * P, :].rearrange("(m p) s -> p m s", p=P), in_=res01[:].rearrange("p (m s) -> p m s", m=2)
                )
            if m == 2:
                nc.sync.dma_start(out=out[rows, :], in_=res[:])
